import numpy as np, ml_dtypes
CORES = [35,38,43,46]
N = 4
BF = ml_dtypes.bfloat16
L, WX, W, FD, RO = 256, 4096, 4096, 256, 4
LW = 12
WT = 2 * np.arange(16) + 1
KINDS = np.array([[16, 0, 0, 0], [15, 1, 0, 0], [8, 8, 0, 0], [4, 4, 4, 4], [13, 1, 1, 1], [7, 6, 2, 1], [14, 2, 0, 0], [6, 5, 5, 0]])
SEQ = np.stack([np.repeat(np.arange(4), a) for a in KINDS])
def move(a):
    return np.roll(a, 1, axis=0)
def pack(X, C, M, S, Z):
    return {"x0": np.ascontiguousarray(X.reshape(N, 128, WX)).astype(np.float32).astype(BF), "cm": np.ascontiguousarray((W * M + C).reshape(N, 128, W)).astype(np.int32),
            "s0": np.ascontiguousarray(S.reshape(N, 128, L)).astype(np.int32), "z0": np.ascontiguousarray(Z.reshape(N, 128, L)).astype(np.float32).astype(BF)}
def parts(rng):
    X = rng.integers(0, 256, (N, 8, 16, WX)); C = rng.integers(0, W, (N, 8, 16, W)); M = rng.integers(0, W, (N, 8, 16, W))
    share = rng.choice(np.array([0.1, 0.3, 0.6]), (N, 8, 1, 1)); pool = rng.integers(0, W, (N, 8, 1, 64))
    few = np.take_along_axis(pool, rng.integers(0, 64, (N, 8, 1, 16 * W)), 3).reshape(N, 8, 16, W)
    C = np.where(rng.random(C.shape) < share, few, C)
    return X, C, M, rng.integers(0, W, (N, 8, 16, L)), rng.integers(0, 256, (N, 8, 16, L))
def classes(rng, kinds):
    s = np.take_along_axis(np.argsort(rng.random((L, 4)), axis=1), SEQ[kinds], 1)
    return np.take_along_axis(s, np.argsort(rng.random((L, 16)), axis=1), 1).T
def juries(rng, X, C, S, Z, q, g, cl):
    v = rng.permutation(W); off = rng.integers(0, W, 16); kind = int(rng.integers(0, 4))
    C[q, g] = v[(np.arange(W)[None, :] + off[:, None]) % W]
    base = np.zeros(16, np.int64) if kind == 0 else np.full(16, 255) if kind == 1 else rng.integers(0, 256, 16)
    Z[q, g] = base[np.argsort(rng.random((16, L)), axis=0)]
    u = int(np.add.reduce(base)); h = (((v * (u + 1)) >> 5) + v) & (WX - 1)
    b = np.add.reduce(X[q, g][:, h] * WT[:, None], axis=0) & 3
    start = rng.integers(0, W, (1, L))
    for c in range(4):
        m = (cl == c).astype(np.int64); before = np.add.accumulate(m, axis=0) - m
        pl = np.flatnonzero(b == c)
        if len(pl) == 0: pl = np.arange(W)
        S[q, g] = np.where(m == 1, (pl[(start + before) % len(pl)] - off[:, None]) % W, S[q, g])
    return off
def setup_inputs(rng):
    return pack(*parts(rng))
def setup_inputs_spread(rng):
    def uneven(n, hi, *shape):
        return np.minimum((hi * rng.random((N, 8, 16, n)) ** rng.choice(np.array([0.125, 0.5, 1.0, 2.0, 5.0]), shape)).astype(np.int64), hi - 1)
    return pack(uneven(WX, 256, N, 8, 1, WX), uneven(W, W, N, 8, 1, 1), uneven(W, W, N, 8, 16, 1), uneven(L, W, N, 8, 1, L), uneven(L, 256, N, 8, 1, L))
def setup_inputs_ends(rng):
    p = np.array([0.0, 0.1, 0.5, 0.9, 1.0])
    X = 255 * (rng.random((N, 8, 16, WX)) < rng.choice(p, (N, 8, 1, WX))).astype(np.int64)
    C = (W - 1) * rng.integers(0, 2, (N, 8, 16, W)); S = (W - 1) * rng.integers(0, 2, (N, 8, 16, L))
    Z = 255 * (rng.random((N, 8, 16, L)) < rng.choice(p, (N, 8, 1, L))).astype(np.int64)
    Z[..., L - 1] = 255; Z[..., 0] = 255; Z[..., 1] = 0; Z[..., L - 2] = 0
    C[:, :, 15, W - 1] = W - 1; S[:, :, 15, L - 1] = W - 1; S[:, :, 15, 0] = W - 1
    X[:, 0] = X[:, 0, :1]
    X[:, :, :, WX - 1] = 255; X[:, ::2, :, 0] = 255; X[:, 1::2, :, 0] = 0
    C[:, 7, :, W - 1] = W - 1; S[:, 7, :, L - 1] = W - 1; S[:, 7, :, 2] = W - 1
    C[:, 5, :, 0] = 0; C[:, 5, :, W - 1] = W - 1
    S[:, 5] = (W - 1) * (np.arange(16)[:, None] == rng.integers(0, 16, (N, 1, L)))
    Z[:, 5] = np.where(Z[:, 5, :1] > 0, 255, 0)
    X[:, 5, :, (613 * np.arange(15)) & (WX - 1)] = 0
    for u in (0, 4080):
        h = ((((W - 1) * (u + 1)) >> 5) + W - 1) & (WX - 1)
        X[:, 5, :, h] = 0; X[:, 5, 0, h] = 255
    M = np.where(rng.random(C.shape) < 0.8, C, W - 1 - C)
    return pack(X, C, M, S, Z)
def setup_inputs_corners(rng):
    X, C, M, S, Z = parts(rng)
    for q in range(N):
        for g in range(8):
            off = juries(rng, X, C, S, Z, q, g, classes(rng, rng.integers(0, 8, L)))
            w = rng.random(L); c = rng.integers(0, W, L)
            S[q, g] = np.where((w < 0.15)[None, :], (c[None, :] - off[:, None]) % W, S[q, g])
            S[q, g, 15] = np.where(w > 0.8, (S[q, g, 0] + off[0] - off[15]) % W, S[q, g, 15])
    return pack(X, C, M, S, Z)
def setup_inputs_crowd(rng):
    X, C, M, S, Z = parts(rng)
    for q in range(N):
        for g in range(8):
            w = (g + q) % 8; kinds = np.full(L, (1, 1, 0, 5, 5, 6, 3, 4)[w]); one = int(rng.integers(0, L))
            if w == 1: kinds[one] = 0
            off = juries(rng, X, C, S, Z, q, g, classes(rng, kinds))
            if w == 3: S[q, g] = S[q, g, :, :1].copy()
            if w == 4: S[q, g] = ((int(rng.integers(0, W)) - off) % W)[:, None]
            if w == 5:
                mine = S[q, g, :, one].copy(); S[q, g] = S[q, g, :, (one + 1) % L].copy()[:, None]; S[q, g, :, one] = mine
    return pack(X, C, M, S, Z)
def setup_inputs_tops(rng):
    X, C, M, S, Z = parts(rng)
    X[:, 1::2] = 255 - (rng.random((N, 4, 16, WX)) < 0.25).astype(np.int64)
    C = np.where(rng.random(C.shape) < 0.5, rng.choice(np.array([W - 17, W - 5, W - 3, W - 1]), C.shape), rng.integers(W - 96, W, C.shape))
    lack = rng.integers(0, 17, (N, 8, 1, L)); lack[..., 0::4] = 4; lack[..., 1::4] = 6; lack[..., 2::4] = 0; lack[..., L - 1] = 4
    Z = 255 - (np.argsort(rng.random((N, 8, 16, L)), axis=2) < lack).astype(np.int64)
    C[:, :, 15, W - 1] = W - 5; S[:, :, 15, L - 1] = W - 1
    return pack(X, C, M, S, Z)
def check_inputs(d):
    bad = []
    for k, hi in (("x0", 255), ("cm", W * W - 1), ("s0", W - 1), ("z0", 255)):
        a = np.asarray(d[k]).astype(np.float64)
        if not (np.min(a) >= 0 and np.max(a) <= hi): bad.append("range of " + k)
        elif np.any(a != np.floor(a)): bad.append("whole numbers in " + k)
    return bad
def reference(x0, cm, s0, z0):
    X = x0.astype(np.float32).astype(np.int64).reshape(N, 8, 16, WX); both = cm.astype(np.int64).reshape(N, 8, 16, W)
    C = both & (W - 1); M = both >> LW
    S = s0.astype(np.int64).reshape(N, 8, 16, L); Z = z0.astype(np.float32).astype(np.int64).reshape(N, 8, 16, L)
    A = np.zeros((N, 8, 1, 1), np.int64); k = np.arange(16); lane = np.arange(L); less = (k[:, None] > k[None, :])[:, :, None]
    for t in range(RO):
        e = np.take_along_axis(C[:, :, (k + t) & 15], S, 3)
        same = (e[:, :, :, None, :] == e[:, :, None, :, :]) & less
        o = np.add.reduce(same.astype(np.int64), axis=3)
        u = np.add.reduce(Z, axis=2)[:, :, None, :]
        h = (((e * (u + 1)) >> 5) + e + 613 * o + A) & (WX - 1)
        x = np.take_along_axis(X, h.reshape(N, 8, 1, 16 * L), 3).reshape(N, 8, 16, 16, L)
        b = np.add.reduce(x * WT[:, None, None], axis=2) & 3
        count = np.stack([np.add.reduce((b == c).astype(np.int64), axis=2) for c in range(4)], axis=2)
        best = np.argmin(np.where(count == 0, 99, count), axis=2)[:, :, None, :]
        sv = b == best; si = sv.astype(np.int64)
        ns = np.add.reduce(si, axis=2)[:, :, None, :]; before = np.add.accumulate(si, axis=2) - si
        place = np.where(sv, before, ns + k[:, None] - before)
        order = np.zeros_like(e); np.put_along_axis(order, place, e, 2)
        first = np.argmax(sv, axis=2)[:, :, None, :]
        hf = np.take_along_axis(h, first, 2); xf = np.take_along_axis(x, first[:, :, None], 3)[:, :, :, 0]
        y = np.take_along_axis(M, e.reshape(N, 8, 1, 16 * L), 3).reshape(N, 8, 16, 16, L)
        Z = np.maximum.reduce(np.where(sv[:, :, None], x, 0), axis=3)
        S = np.maximum.reduce(np.where(sv[:, :, None], y, 0), axis=3)
        np.put_along_axis(C, np.broadcast_to((W // L) * lane + (u & (W // L - 1)), (N, 8, 16, L)), order, 3)
        np.put_along_axis(X, np.broadcast_to(hf - (hf & (L - 1)) + lane, (N, 8, 16, L)), (xf + Z) >> 1, 3)
        A = np.add.reduce((ns == 1).astype(np.int64), axis=3)[..., None]
        if t < RO - 1:
            S = move(S); Z = move(Z)
    yx = np.add.reduce(X.reshape(N, 128, WX // FD, FD) * np.arange(1, WX // FD + 1)[:, None], axis=2)
    yc = np.add.reduce(C.reshape(N, 128, W // FD, FD) * np.arange(1, W // FD + 1)[:, None], axis=2)
    return {"yx": yx.astype(np.float32), "yc": yc.astype(np.float32), "ys": np.ascontiguousarray(S).reshape(N, 128, L).astype(np.float32), "yz": np.ascontiguousarray(Z).reshape(N, 128, L).astype(np.float32).astype(BF)}

@@ -1,0 +1,782 @@
+import numpy as np
+from concourse.mybir import AluOpType as OP, ActivationFunctionType as AF
+
+LEVELS, H, n = 4, 2, 128
+F32, BF, F16, I32, U16 = "float32", "bfloat16", "float16", "int32", "uint16"
+SB = {
+    "mt": (4104, I32), "ct": (4096, I32), "xt": (4096, BF), "s0i": (256, I32),
+    "gw": (4096, F16), "xw": (4128, BF), "es": (256, F16), "u1": (256, F32), "eq": (2048, F16),
+    "p1": (256, F32), "p2": (256, I32), "hh": (256, I32), "h16": (256, U16), "hi": (256, BF),
+    "ti": (256, I32), "bb": (256, BF), "ind": (768, BF), "sg": (256, BF), "sr": (256, BF), "sv": (256, BF),
+    "t1": (256, BF), "rr": (2 * 1920, F32), "ft": (256, F32), "fv": (256, I32), "l2": (48, U16),
+    "ui": (16, I32), "uj": (16, I32), "lc": (16, U16), "xa": (1024, F16), "xs": (1024, F16), "yl": (256, U16),
+    "ya": (1024, F32), "yw": (4096, F32), "yn": (4096, F32), "si": (256, I32), "sj": (256, I32),
+    "zq": (8 * 384, BF), "su": (1024, U16), "zs": (1024, BF), "ss": (768, U16), "ysf": (256, F32),
+    "junk": (256, BF), "acol": (8, F32), "da": (128, F16), "oyx": (256, F32), "oyc": (256, F32),
+    "ones": (256, BF), "idf": (128, F32), "ib": (128, BF), "i32": (128, BF), "i4k": (128, BF), "ob": (128, BF),
+    "o2k": (128, BF), "lo": (128, BF), "l4k": (128, BF), "b1": (128, BF), "qa": (128, BF), "fi": (128, BF),
+    "wd": (2304, BF), "o1": (144, BF), "bw": (144, BF), "dm": (1024, BF), "ad": (1024, F16), "rs": (2048, BF),
+    "yp": (576, BF), "mi": (2048, BF), "sm": (96, F32), "raw": (64, F32), "pm": (16, F32), "r0": (1024, BF),
+    "tie": (80, F32), "im": (128, BF), "pos": (128, F16), "xl": (256, U16), "xm": (4096, BF), "xn": (4096, BF), "qi": (4, I32), "qf": (16, F32), "dd": (8, F32),
+    "tau": (24, F32), "a16": (8, F32), "rx": (512, BF), "r16": (1024, BF),
+}
+SCRATCH = {k: ("sbuf", [128, v[0]], v[1]) for k, v in SB.items()}
+SCRATCH["stat"] = ("sbuf", [128, 6, 8], BF)
+SCRATCH["zz"] = ("sbuf", [128, 8, 32], BF)
+SCRATCH["st"] = ("sbuf", [128, 6, 8, 16], F16)
+for _b in range(8):
+    SCRATCH["ps%d" % _b] = ("psum", [128, 32, 16], F32)
+SEMAPHORES = (["V", "S", "P", "G", "left"] + ["ar%d" % i for i in range(12)] + ["d%d" % i for i in range(24)])
+DRAM = {"x0": (4096, BF), "cm": (4096, I32), "s0": (256, I32), "z0": (256, BF),
+        "yx": (256, F32), "yc": (256, F32), "ys": (256, F32), "yz": (256, BF)}
+ALL = slice(None)
+COLS = {}
+
+CFG = {
+    "ymode": "AAAAAAAB",
+    "xmode": "AAAAAAAB",
+    "eng": {},
+    "seed": 1, "jit": 0.0, "delta": 200.0, "xbanks": 2, "ne": 8, "gp": 4, "order": None,
+}
+CFG.update({
+    "ymode": "ABABABAB", "xmode": "BABABABA",
+    "order": "030j241l1p0s0v0x0w251z1t1w1q1u1r0t0p280y1k040q1j2x39200k0u0r1s0o1n0l050m100n171m311o2e2f1v29181x1a21191y06161f221c2608231b1i0f0e2z2a09000z1g024t272b0g1e2d3l1d1h2c0a14013u2q133a2u2g2h120d0b0c113o4u3p3n3q150i0h4n3r3s3t3x3z403y074m3v4q4p4o41373w3b4243442w2i2s2v2j4r4s474w464y4z4x324v3c3e4a2y48492p35502k51332l524b2m2t532n554c4d4f4e3d3f583g4g564h4i594j4k57453j5a4l3h5b5c36543k30345d5e3m5l6v5m2r6w765f3i77615g73785h5n625i5j5k79746x6l657u7m7v71727a7k636667687w697b5o6z5p6m6n6p5q826a7y6q7c6s7d6y6t70837z7x5t5r5s6b6c5u6e5v5w7e5x6d5y806f75816g6h6i2o5z606r6j6k6u7j7l7n8c7o7p7g84648f6o7f7q8j8d7r7h8a8e8g8h7s8k8b7i857t8i8m8o878l8n8p8q9d8r889c9b869e8s8t899f8v9g9h9n8x9i9l8w9j8y8z908u9m9o9192949p93959k96979q9r389s9v9t98999a9uaqbk9w9xaabl9yarbm9za0a1abacada3bvbsbobqa2aebnafbwbxa4a5a6bpa7bra8a9baauagavbbahbcasaibybzajawakaxayc0cjckbeazclbfbgc1alamb0anb3aob1b2apcpb4b5b6b7cnc9btbubhc2b8cbcrcmbibjcscqcoc3b9cactatcdc4c8ccbdd2ced1c5cfd3d4cgc6chczcid5d6cuc7d8d7dbd9cvddcwd0dadcdee2e0e3dfe1dgcxe4dhdicydke5e6dldmdne7eaecdodpedebeee8dqdrdte9dsdudvefegeheidwdxekejdydzg9ezdjemffengagbeleofgf0epeqeserfhgfgkgcgleteugmf1f2evewexggeyfjgnf3gdfzh8h9gof4fkhcg0gyf5gphgflgqf8h0g1g3g4g6f7f6gzfmfnhafog5f9fah2fsh1g7hdgrfphbhhfbfqhehfgsfrg2fch4ftfufvh3gehifdfwfehjfifxfyg8gxh5ghhrhqgihogjh6guhshugthth7hkhvisgvhwipiqi2hlgwi0i3i1irithxhpiuhyi4iviziwhmhzixhni5i6i7j1j0j2iyiaj3i9j4icidj5j6ibj9iej8ifjcjbjai8igihiiijikiliminiojdjojpk4kwjejqjfjhjgj7kxjijrjsjjk5k6jtl2jul0l7jkl8jll4jxjmkyjnjyknk7kolulskpl9k8l1kzl3jvjwlaltl5lvm2kqkrk9jzkakbk0ksl6k1ktlwlyk2kckglhkulilxk3lzkdkhlbm0kekim3lgkfmam6kjkkklljkvm1lomfkmmglrm4mhmmm7lplcmnldmelqlembm5molflkmilmlllnmjmkm8mlm9mcmpmqmd",
+})
+CFG.update({
+    "order": "0s0u1p0j28031w040t0x1z1x0w1t0v0k1q0y392x1n171l180p1y1r0q2e0o10112420190e1u2113050r3a0n291s1v2a1a0z1j1m2w1e08311k2f220f06262z2q231d1c25092d2b14000m0102162u0g1i1h271f2c0a0b0l1o3u2g0d0c2h4t1b1g123o3p0h0i3n3r153q4n3v3s3t4u3z4m073x4p404o2p4q3l3y2i2y3w412j3b4243442v3d4r374s4y4w464z4x323e4v472s354a3c495051482k2l4b33453f523g4c2m2n532t4d4f4e554g583m564h4i4j594k573j5a36544l6v6w3h5b30765l5c3k736z5d5e5f5g2r345h777461785i5m5j3i5k5n656l797u66677k6x717262635o5p645q6m6n6y707a7v6p7b7w7m6q7c5u5r68695s6a6s5t5v7d5w7y6t757x6b6c6e7e5x6f827z835y6d6g807f5z6h816i606u6o6j6k7j8a847l6r8d8e8f8j7n7o8c7p7q857g7r8g8k2o8b8h8i8m7h7s7t869b9c7i8o878n8p888l898q8r8s8t9e9d9f9g8v9i8x8w9h9l9j8y9n8z909k9m9o919p9293949q9r9s8u95969v979t98999aaqbk9u9w9xblaaab38ar9ybm9za0acadbsa1a2a3aeafbva4a5bobqbwa6bna7bxbpbrbtajasa8a9ahauavcjbybackawagakalbzaxc0ayc1buaiamanbbbcbeclcmazb1aob3c9b0b4b5apb2cpcnb6bfb7b8atcabgbdc2bhcrcbbicsbjcqcoc3ctb9c8d1d4cdc4ccc5d2c6cucfd3ced5d6d7c7cgczchd8d9dbddd0dadcdecicwe3dfe0cve1e2dgcxdhdicye4dke5e6ecdldmdneadoe7e8dpebeddqdrdtdse9eeefegehdjdudvejeidwdxdyekdzffg9enelemgaeogbezgkfgfhgfepeqeresgletgcf0euf1evgmf2ewexggeyfjfzh8gngoh9f3gdfkflh0gyf4g0g1fmfnhagpgzfofpf7frf6gqg3f5g4grfsh2f8fthghbgef9h1hhhefqg6hffahcfbfufifvhdfcg7g2fdfwfxgsh4hifeh3g5g8fyhjgxghhqgihrh5gjhshuguh6gvgth7hthkipiqhvishwhoi0gwhli2i3i1hmirithxiuhphyhzi4ivhni5iziwi6j0j1j2ixi7ibj3iyiaj4j5j6j9i9idicieifj8igjcihiiijjbjaikilj7iminjdioi8jojpjejfjhjgkwkxk4k5k6jqjijrjsjtl7kyjul8jjjkl2kzjll9jxjmjwjyjnjvk7knk8lsjzlukol4kpltl0l3lal5l1k9lvl6kakbkckqkrlwksk0k1kdlylxm2m3lgk2lhktkflzlikekgkhkim0k3maljm6kjlokkklkum1kvmflbkmmglrmhm4lclplkllmemmm5ldlqlmmimnlem7mblfmomkm8m9lnmcmjmlmpmqmd",
+    "engs": "000180eb04704b6c010040f3882ac02ce71582b02448130255f9088142588a13c493c18028e48412",
+})
+COST = {"f": 1.2, "cyc": 0.83, "pe": 0.417, "r": 1.56, "sc": 3.8, "vfix": 60.0, "sfix": 75.0, "pfix": 30.0,
+        "wake": 100.0, "own": 60.0, "bw": 220.0, "dlat": 1800.0, "send": 1000.0, "slat": 3000.0, "tt2": 2.0}
+
+
+def ap(name, a=None, b=None, s=None):
+    return ("ap", name, (ALL, slice(a, b, s)))
+
+
+def ap3(name, i, j, part=ALL):
+    return ("ap", name, (part, i, j))
+
+
+def ps(tile, a, b):
+    return ("ap", tile, (ALL, slice(a // 16, b // 16), ALL))
+
+
+def ind(win, off):
+    return ("ind", win, off)
+
+
+def shape_of(name):
+    if name.startswith("P:"):
+        return [128, 32, 16], F32
+    if name in DRAM:
+        return [128, DRAM[name][0]], DRAM[name][1]
+    return SCRATCH[name][1], SCRATCH[name][2]
+
+
+def cols(a):
+    key = ("P:" if a[1].startswith("P:") else a[1], str(a[2]))
+    if key not in COLS:
+        sh = shape_of(a[1])[0]
+        COLS[key] = np.arange(int(np.prod(sh[1:]))).reshape(sh[1:])[a[2][1:]].reshape(-1)
+    return COLS[key]
+
+
+def isap(a):
+    return isinstance(a, tuple) and len(a) == 3 and a[0] in ("ap", "ind")
+
+
+def two(a):
+    return shape_of(a[1])[1] in (BF, F16, U16)
+
+
+def call_cost(c, K):
+    k = c[0]
+    cy = K["cyc"] * K["f"]
+    if k == "mm":
+        N, M = len(cols(c[3])), len(cols(c[2]))
+        return max(min(64, M), N) * (4 if shape_of(c[2][1])[1] == F32 else 1) * K["pe"] * K["f"]
+    if k == "iota":
+        return 130 + 2 * len(cols(c[1])) * cy
+    if k == "sel":
+        return 170 + 2 * len(cols(c[1])) * cy
+    if k == "dma":
+        return 128 * len(cols(c[1])) * (2 if two(c[1]) else 4) / K["bw"]
+    if k == "send":
+        return K["send"]
+    fix = K["sfix"] if k == "act" else K["vfix"]
+    aps = [a for a in c[1:] if isap(a)]
+    if c[1][0] == "ind":
+        return fix + 16 * len(cols(c[1][2])) * K["sc"] * cy
+    m = len(cols(c[1]))
+    if any(a[0] == "ind" for a in aps):
+        return fix + m * K["r"] * cy
+    if k == "act":
+        return fix + max(64, m) * cy
+    if k == "tt":
+        both = not (c[2][1].startswith("P:") or c[3][1].startswith("P:"))
+        return fix + max(64, m * (K["tt2"] if both else 1)) * cy
+    wide = [a for a in aps if len(cols(a)) > 1]
+    return fix + max(64, m * (0.5 if all(two(a) for a in wide) else 1)) * cy
+
+
+def build(cfg):
+    ops = []
+    cfg["free"] = {}
+
+    def op(name, eng, *calls):
+        ops.append({"name": name, "eng": eng, "calls": list(calls)})
+
+    def eng(name, dflt):
+        cfg["free"][name] = dflt
+        if cfg.get("engs"):
+            k = len(cfg["free"]) - 1
+            return "V" if int(cfg["engs"][k // 4], 16) >> (3 - k % 4) & 1 else "S"
+        return cfg["eng"].get(name, dflt)
+
+    def lin(name, dflt, out, in_, scale=1.0, bias=0.0, relu=False):
+        if eng(name, dflt) == "S":
+            op(name, "S", ("act", out, in_, AF.Relu if relu else AF.Identity, bias, scale, None))
+        elif relu and shape_of(out[1])[1] != U16:
+            assert scale == 1.0
+            op(name, "V", ("ts", out, in_, bias, 0.0, OP.add, OP.max))
+        elif scale == 1.0 and not isap(bias) and bias == 0.0:
+            op(name, "V", ("copy", out, in_))
+        elif scale == 1.0:
+            op(name, "V", ("ts", out, in_, bias, None, OP.add, None))
+        else:
+            op(name, "V", ("ts", out, in_, scale, bias, OP.mult, OP.add))
+
+    def ts(name, out, in_, s1, s2, o0, o1=None):
+        op(name, "V", ("ts", out, in_, s1, s2, o0, o1))
+
+    def tt(name, out, a, b, o):
+        op(name, "V", ("tt", out, a, b, o))
+
+    def fill(name, out, v):
+        op(name, "V", ("memset", out, v))
+
+    def mms(name, lst, first=True, last=True):
+        op(name, "P", *[("mm", o, l, r, first and i == 0, last and i == len(lst) - 1) for i, (o, l, r) in enumerate(lst)])
+
+    def col(j):
+        return ap("qf", j, j + 1)
+
+    op("ld.s", "A", ("dma", ap("s0i"), ap("s0")))
+    for h in range(H):
+        op("ld.z%d" % h, "A", ("dma", ap("zq", 384 * h + 256, 384 * h + 384), ap("z0", n * h, n * h + n)))
+    NC = cfg.get("nc", 4)
+    w = 4096 // NC
+    for j in range(NC):
+        op("ld.c%d" % j, "Y", ("dma", ap("mt", 8 + w * j, 8 + w * j + w), ap("cm", w * j, w * j + w)))
+    op("ld.x", "Y", ("dma", ap("xt"), ap("x0")))
+    for j in range(NC):
+        ts("c%d" % j, ap("ct", w * j, w * j + w), ap("mt", 8 + w * j, 8 + w * j + w), 4095, None, OP.bitwise_and)
+    for h in range(H):
+        lin("su0.%d" % h, "S", ap("su", n * h, n * h + n), ap("s0i", n * h, n * h + n))
+    fill("m0", ap("mt", 0, 8), 0)
+    for j in range(NC):
+        ts("m%d" % (j + 1), ap("mt", 8 + w * j, 8 + w * j + w), ap("mt", 8 + w * j, 8 + w * j + w), 12, None, OP.logical_shift_right)
+
+    def sel(name, out, in_, pat, cmp, base, ch):
+        op(name, "G", ("sel", out, in_, pat, cmp, 0.0, base, ch))
+
+    def diag(name, out, in_, v):
+        op(name, "G", ("sel", out, in_, [[-1, 128]], OP.not_equal, v, 0, 1))
+
+    def iota(name, out, pat, base, ch):
+        op(name, "G", ("iota", out, pat, base, ch))
+
+    fill("k.ones", ap("ones"), 1.0)
+    fill("k.wd0", ap("wd"), 1.0 / 4096)
+    for j in range(2):
+        sel("k.wd%d" % (j + 1), ap("wd", 1152 * j, 1152 * j + 1152), ap("wd", 1152 * j, 1152 * j + 1152),
+            [[-1, 8], [-16, 9], [1000, 16]], OP.is_equal, -15000 - 8 * j, 1)
+    sel("k.ib", ap("ib"), ap("ones", 0, 128), [[-1, 128]], OP.is_equal, 0, 1)
+    sel("k.zz", ap3("zz", ALL, ALL), ap("ones"), [[-16, 8], [0, 2], [-1, 16]], OP.is_equal, 0, 1)
+    sel("k.ob1", ap("ob"), ap("ones", 0, 128), [[-16, 8], [0, 16]], OP.is_ge, 0, 1)
+    sel("k.ob2", ap("ob"), ap("ob"), [[16, 8], [0, 16]], OP.is_ge, 15, -1)
+    sel("k.lo", ap("lo"), ap("ob"), [[1, 128]], OP.is_gt, 0, -1)
+    iota("k.q", ap("qi", 0, 1), [[0, 1]], 0, 1)
+    iota("k.dd", ap("dd"), [[1, 8]], 1, 0)
+    iota("k.im", ap("im"), [[1, 128]], 0, 0)
+    ts("k.q1", ap("qi", 1, 2), ap("qi", 0, 1), 15, None, OP.bitwise_and)
+    ts("k.q2", ap("qi", 2, 3), ap("qi", 0, 1), 2, 3, OP.logical_shift_right, OP.bitwise_and)
+    ts("k.q3", ap("qi", 3, 4), ap("qi", 0, 1), 3, None, OP.bitwise_and)
+    lin("k.qf", "V", ap("qf", 0, 4), ap("qi"))
+    for d in range(1, 9):
+        diag("k.dm%d" % d, ap("dm", 128 * d - 128, 128 * d), ap3("zz", ALL, slice(d, d + 16)), -1.0)
+    ts("k.t1", ap("tau", 0, 8), ap("dd"), col(1), 15.0, OP.add, OP.is_le)
+    tt("k.t2", ap("tau", 8, 16), ap("tau", 0, 8), ap("dd"), OP.mult)
+    ts("k.t3", ap("tau", 16, 24), ap("tau", 8, 16), col(0), None, OP.add)
+    ts("k.t4", col(4), ap("tau", 7, 8), 19616.0, None, OP.mult)
+    for d in range(1, 9):
+        ts("k.ad%d" % d, ap("ad", 128 * d - 128, 128 * d), ap("im"), ap("tau", 15 + d, 16 + d),
+           col(4) if d == 8 else 19616.0, OP.is_equal, OP.mult)
+    lin("k.o2k", "S", ap("o2k"), ap("ob"), 2048.0)
+    lin("k.da", "S", ap("da"), ap("ones", 0, 128), -15856.0)
+    fill("k.o10", ap("o1"), 0.0)
+    lin("k.o1", "S", ap("o1", 15, 143, 16), ap("ob", 0, 128, 16))
+    lin("k.w", "S", col(5), col(0), 0.5, 0.25)
+    op("k.bw", "S", ("act", ap("bw"), ap("o1"), AF.Identity, 0.0, col(5), None))
+    fill("k.s0", ap("raw"), 0.0)
+    for j in range(4):
+        fill("k.sa%d" % j, ap("raw", 17 * j, 16 * j + 16, 4), 16.0)
+        fill("k.sb%d" % j, ap("raw", 20 * j, 20 * j + 4), -16.0)
+        fill("k.sc%d" % j, ap("raw", 21 * j, 21 * j + 1), 4.0)
+    tt("k.sd", ap("sm", 32, 80), ap("raw", 16, 64), ap("raw", 0, 48), OP.subtract)
+    tt("k.se", ap("sm", 0, 32), ap("sm", 48, 80), ap("sm", 32, 64), OP.subtract)
+    iota("k.tie", ap("tie", 0, 16), [[-2, 4], [2, 4]], -1, 0)
+    lin("k.tie2", "S", ap("tie", 0, 16), ap("tie", 0, 16), 1.0 / 32)
+    lin("k.sh", "S", ap("tie", 16, 32), ap("raw", 0, 16), 0.25)
+    tt("k.sf", ap("sm", 48, 64), ap("tie", 0, 16), ap("tie", 16, 32), OP.add)
+    iota("k.m4", ap("tie", 64, 80), [[1, 4], [0, 4]], 0, 0)
+    tt("k.dq", col(6), col(2), col(3), OP.is_equal)
+    lin("k.dq2", "S", col(11), col(6), 4.0, 1.0)
+    ts("k.s2a", ap("sm", 64, 80), ap("tie", 64, 80), col(2), col(11), OP.is_equal, OP.mult)
+    ts("k.s2b", ap("sm", 64, 80), ap("sm", 64, 80), col(6), None, OP.subtract)
+    ts("k.s3", ap("sm", 80, 96), ap("ones", 0, 16), col(2), 1.0 / 16, OP.mult, OP.mult)
+    lin("k.pm0", "S", ap("pm", 0, 16, 2), ap("ob", 0, 128, 16), -1.0)
+    lin("k.pm1", "S", ap("pm", 1, 16, 2), ap("ob", 0, 128, 16))
+    for j in range(8):
+        op("k.sx%d" % j, "S", ("act", ("ap", "st", (ALL, ALL, j, ALL)), ap("sm"), AF.Identity, 0.0, ap("pm", 2 * j + 1, 2 * j + 2), None))
+    lin("k.i32", "S", ap("i32"), ap("ib"), 32.0)
+    lin("k.i4k", "S", ap("i4k"), ap("ib"), 4096.0)
+    lin("k.l4k", "S", ap("l4k"), ap("lo"), 4096.0)
+    lin("k.idf", "S", ap("idf"), ap("ib"))
+    lin("k.qa0", "S", ap("qa"), ap("lo"), -4096.0)
+    diag("k.qa1", ap("qa"), ap("qa"), 4096.0)
+    lin("k.b10", "S", ap("b1"), ap("lo"), -2.0)
+    diag("k.b11", ap("b1"), ap("b1"), -32.0)
+    lin("k.fi", "S", ap("fi"), ap("o1", 15, 143), 4096.0)
+    lin("k.k16", "S", col(7), col(1), 1.0, -16.0)
+    ts("k.fb0", col(8), col(1), 0.0, 524288.0, OP.is_equal, OP.mult)
+    lin("k.fb1", "S", col(9), col(1), 4096.0, -61440.0)
+    tt("k.fb2", col(10), col(8), col(9), OP.add)
+    lin("k.a16", "S", ap("a16"), ap("dd"), 16.0, -16.0)
+    fill("k.st0", ap3("stat", ALL, ALL), 0.0)
+    for h in range(H):
+        ts("k.st1%d" % h, ap3("stat", 3 * h, ALL), ap("a16"), col(1), 128.0 * h, OP.add, OP.add)
+        ts("k.st2%d" % h, ap3("stat", 3 * h + 1, ALL), ap("a16"), col(1), 16.0, OP.add, OP.mult)
+    if "B" in cfg["xmode"]:
+        for h in range(H):
+            fill("k.xz%d" % h, ap("xw", 2064 * h, 2064 * h + 16), 0.0)
+        lin("k.pos0", "S", col(12), col(1), 1.0, -1024.0)
+        lin("k.pos1", "S", ap("pos"), ap("im"), 16.0, col(12))
+    fill("k.rs0", ap("r0"), 256.0)
+    for j in range(2):
+        sel("k.rs%d" % (j + 1), ap("rs", 1024 * j, 1024 * j + 1024), ap("r0"), [[-1, 8], [-16, 8], [0, 16]], OP.is_equal, -8 * j, 1)
+    lin("k.yp0", "S", ap("yp"), ap("r0", 0, 576), 1.0 / 256)
+    sel("k.yp1", ap("yp"), ap("yp"), [[-4, 4], [-16, 9], [-1, 16]], OP.is_equal, 12, 1)
+    sel("k.yp2", ap("yp"), ap("yp"), [[0, 36], [1, 16]], OP.is_ge, -12, 0)
+    lin("k.rx0", "S", ap("rx"), ap("r0", 0, 512), 1.0 / 256)
+    lin("k.rx1", "S", ap("rx", 0, 512, 4), ap("r0", 0, 128), 0.0)
+    if "B" in cfg["ymode"] + cfg["xmode"]:
+        lin("k.r160", "S", ap("r16"), ap("r0"), 1.0 / 256)
+        lin("k.r161", "S", ap("r16", 0, 1024, 16), ap("r0", 0, 64), 0.0)
+    iota("k.mi0", ap("mi"), [[1, 16], [0, 128]], 1, 0)
+    sel("k.mi1", ap("mi"), ap("mi"), [[0, 16], [-1, 128]], OP.is_equal, 0, 1)
+
+    GP = cfg["gp"]
+    gl = n // GP
+
+    def xw(h, a=0, b=2048, s=None):
+        return ap("xw", 2064 * h + 16 + a, 2064 * h + 16 + b, s)
+
+    def st(j):
+        return ("ap", "st", (ALL, j, ALL, ALL))
+
+    def c(name, h, m=1, a=0, b=None):
+        return ap(name, m * n * h + a, m * n * h + (m * n if b is None else b))
+
+    for t in range(LEVELS):
+        last = t == LEVELS - 1
+        for h in range(H):
+            x = ".%d%d" % (t, h)
+            zb = 384 * (2 * t + h)
+            z = ap("zq", zb + 256, zb + 384)
+            for j in range(GP):
+                lin("g1" + x + str(j), "S", c("gw", h, 16, 16 * gl * j, 16 * gl * (j + 1)),
+                    ind(ap("ct"), ap("su", 256 * t + n * h + gl * j, 256 * t + n * h + gl * j + gl)), 1.0, -2048.0)
+            pe = ps("P:e" + x, 0, n)
+            for j in range(2):
+                mms("d1" + x + str(j), [(ps("P:e" + x, 64 * j, 64 * j + 64), ap("wd", 144 * ((k + t) & 15) + 15 - k, 144 * ((k + t) & 15) + 143 - k),
+                                         ap("gw", 2048 * h + 1024 * j + k, 2048 * h + 1024 * j + 1024, 16)) for k in range(16)], j == 0, j == 1)
+            lin("es" + x, "V", c("es", h), pe)
+            pu = ps("P:u" + x, 0, n)
+            mms("u" + x, [(pu, ap("ob"), z)])
+            lin("u1" + x, "S", c("u1", h), pu, 4096.0, 33.0 * 4096)
+            tt("p1" + x, c("p1", h), pe, c("u1", h), OP.mult)
+            for j in range(2):
+                tile = "P:d%d" % j + x
+                mms("df%d" % j + x, [(ps(tile, n * i, n * i + n), ap("dm", 512 * j + 128 * i, 512 * j + 128 * i + 128), c("es", h))
+                                     for i in range(4)])
+                ts("eq%d" % j + x, c("eq", h, 8, 512 * j, 512 * j + 512), ps(tile, 0, 512), 0.0, None, OP.is_equal)
+            pr = ps("P:r" + x, 0, n)
+            mms("r" + x, [(pr, ap("da"), ap("ones", 0, n)), (pr, ap("o2k"), z)] +
+                [(pr, ap("ad", 128 * d, 128 * d + 128), c("eq", h, 8, n * d, n * d + n)) for d in range(8)])
+            tt("p2" + x, c("p2", h), pr, c("p1", h), OP.add)
+            ts("hh" + x, c("hh", h), c("p2", h), 5, 4095, OP.arith_shift_right, OP.bitwise_and)
+            lin("h16" + x, "V", c("h16", h), c("hh", h))
+            lin("hi" + x, "V", c("hi", h), c("hh", h), 1.0, 36736.5)
+            for j in range(GP):
+                lin("g2" + x + str(j), "S", xw(h, 16 * gl * j, 16 * gl * (j + 1)),
+                    ind(ap("xt"), c("h16", h, 1, gl * j, gl * j + gl)))
+            pb = ps("P:b" + x, 0, n)
+            for j in range(2):
+                mms("bn" + x + str(j), [(ps("P:b" + x, 64 * j, 64 * j + 64), ap("bw", 15 - k, 143 - k),
+                                         xw(h, 1024 * j + k, 1024 * j + 1024, 16)) for k in range(16)], j == 0, j == 1)
+            ts("ti" + x, c("ti", h), pb, -0.375, None, OP.add)
+            tt("bb" + x, c("bb", h), pb, c("ti", h), OP.subtract)
+            for j in range(2):
+                lin("i%d" % j + x, "V", c("ind", h, 2, n * j, n * j + n), c("bb", h), 1.0, -0.25 * (j + 1), True)
+            p1 = ps("P:s1" + x, 0, n)
+            mms("s1" + x, [(p1, st(3), ap("ones", 0, n)), (p1, st(2), c("bb", h))] +
+                [(p1, st(j), c("ind", h, 2, n * j, n * j + n)) for j in range(2)])
+            signs = eng("sg" + x, "V") == "S"
+            if signs:
+                op("sg" + x, "S", ("act", c("sg", h), p1, AF.Sign, 0.0, 1.0, None))
+            else:
+                ts("sg" + x, c("sg", h), p1, 0.0, None, OP.is_gt)
+            p2 = ps("P:s2" + x, 0, n)
+            mms("s2" + x, [(p2, st(4), c("sg", h))])
+            if eng("sr" + x, "V") == "S":
+                op("sr" + x, "S", ("act", c("sr", h), p2, AF.Relu, -1.0 if signs else -3.0, 0.5 if signs else 1.0, None))
+            else:
+                ts("sr" + x, c("sr", h), p2, 4.0, None, OP.is_equal)
+            p3 = ps("P:s3" + x, 0, n)
+            mms("s3" + x, [(p3, st(5), c("sr", h))])
+            tt("sv" + x, c("sv", h), p3, c("bb", h), OP.is_equal)
+        for h in range(H):
+            x = ".%d%d" % (t, h)
+            zb = 384 * (2 * t + h)
+            sv, es = c("sv", h), c("es", h)
+            pt = ps("P:t" + x, 0, n)
+            mms("t" + x, [(pt, ap("ob"), sv), (pt, ap("b1"), sv)])
+            lin("t1" + x, "S", c("t1", h), pt, 1.0, col(1), True)
+            pk = ps("P:k" + x, 0, n)
+            mms("k" + x, [(pk, ap("l4k"), sv), (pk, ap("i4k"), es), (pk, ap("i4k"), c("t1", h))])
+            lin("ra" + x, "S", c("rr", h, 15, 0, n), pk, 1.0, -2048.0, True)
+            lin("rb" + x, "S", c("rr", h, 15, n, 2 * n), pk, 1.0, -6144.0, True)
+            lin("rc" + x, "S", c("rr", h, 15, 2 * n, 4 * n), c("rr", h, 15, 0, 2 * n), 1.0, -8192.0, True)
+            lin("rd" + x, "S", c("rr", h, 15, 4 * n, 8 * n), c("rr", h, 15, 0, 4 * n), 1.0, -16384.0, True)
+            lin("re" + x, "S", c("rr", h, 15, 8 * n, 12 * n), c("rr", h, 15, 0, 4 * n), 1.0, -32768.0, True)
+            lin("rf" + x, "S", c("rr", h, 15, 12 * n, 15 * n), c("rr", h, 15, 0, 3 * n), 1.0, -49152.0, True)
+            tile = "P:f" + x
+            fm = [(ps(tile, 0, n), es, ap("fi"))] + [(ap3(tile, slice(0, 8), slice(p - 1, p + 1)), c("rr", h, 15, n * p - n, n * p), ap("pm"))
+                                                    for p in range(1, 16)]
+            mms("fa" + x, fm[:5], True, False)
+            mms("fb" + x, fm[5:9], False, False)
+            mms("fc" + x, fm[9:13], False, False)
+            mms("fd" + x, fm[13:], False, True)
+            lin("ft" + x, "S", c("ft", h), ps(tile, 0, n))
+            pf = ps("P:g" + x, 0, n)
+            mms("fe" + x, [(pf, c("ft", h), ap("idf"))])
+            lin("fv" + x, "S", c("fv", h), pf, 1.0, col(10))
+            tile = "P:q" + x
+            mms("q" + x, [(ps(tile, 0, n), ap("ib"), c("hi", h)), (ps(tile, 0, n), ap("qa"), sv), (ps(tile, n, 2 * n), ap("qa"), sv)] +
+                ([] if last else [(ps(tile, 2 * n, 3 * n), ap("ob"), sv)]))
+            lin("q1" + x, "S", ap("zq", zb, zb + n), ps(tile, 0, n), 1.0, -40960.0, True)
+            op("q2" + x, "S", ("act", ap("zq", zb + n, zb + 2 * n), ps(tile, n, 2 * n), AF.Relu, col(7), 1.0 / 256, None))
+            if not last:
+                op("ns" + x, "S", ("act", c("junk", h), ps(tile, 2 * n, 3 * n), AF.Relu, 2.0, -1.0, ap("acol", h, h + 1)))
+            if h == 1:
+                tile = "P:l" + x
+                pl = ap3(tile, slice(0, 6), slice(0, 8))
+                mms("l" + x, [(pl, ap("ib"), ap3("stat", ALL, ALL))] +
+                    [(pl, ap("o1", 15 - b, 143 - b), ap("zq", zb - 384 + b, zb + 384, 16)) for b in range(16)])
+                lin("ui" + x, "V", ap("ui"), ap3(tile, slice(2, 6, 3), slice(0, 8)))
+                lin("l2" + x, "V", ap("l2"), pl)
+                ts("uj" + x, ap("uj"), ap("ui"), 15, None, OP.bitwise_and)
+                tt("lc" + x, ap("lc"), ap("uj"), ap3("stat", slice(1, 6, 3), ALL), OP.add)
+        for h in range(H):
+            x = ".%d%d" % (t, h)
+            sv, es = c("sv", h), c("es", h)
+            op("cs" + x, "V", ("copy", ind(c("ct", h, 16), ap("lc", 8 * h, 8 * h + 8)), c("fv", h)))
+            zn = ap("zs", 256 * t + n * h, 256 * t + n * h + n)
+            if cfg["xmode"][2 * t + h] == "B":
+                tile = "P:x" + x
+                mms("x" + x, [(ps(tile, 0, n), ap("ib"), ap("pos")), (ps(tile, 0, n), ap("i4k"), sv)])
+                lin("xl" + x, "S", c("xl", h), ps(tile, 0, n), 1.0, -3056.0, True)
+                for j in range(GP):
+                    part = (h, 16, 16 * gl * j, 16 * gl * (j + 1))
+                    lin("xb%d" % j + x, "S", c("xm", *part), ind(xw(h, -16), c("xl", h, 1, gl * j, gl * j + gl)))
+                    op("xn%d" % j + x, "V", ("scan", c("xn", *part), ap("r16", 0, 16 * gl), c("xm", *part), 0.0, OP.mult, OP.max))
+                lin("zn" + x, "V", zn, ap("xn", 2048 * h + 15, 2048 * h + 2048, 16))
+            for j in range(4 if cfg["xmode"][2 * t + h] == "A" else 0):
+                tile = "P:x%d" % j + x
+                lst = []
+                for s in range(4):
+                    k = 4 * j + s
+                    o = ap3(tile, ALL, slice(s, 16, 4))
+                    lst += [(o, ap("ib"), xw(h, k, 2048, 16)), (o, ap("rs", 128 * k, 128 * k + 128), sv)]
+                mms("x%d" % j + x, lst)
+                if j == 0:
+                    lin("xa0" + x, "S", c("xa", h, 4), ps(tile, 0, 512))
+                else:
+                    tt("xa%d" % j + x, c("xa", h, 4), ps(tile, 0, 512), c("xa", h, 4), OP.max)
+            if cfg["xmode"][2 * t + h] == "A":
+                op("xs" + x, "V", ("scan", c("xs", h, 4), ap("rx"), c("xa", h, 4), 0.0, OP.mult, OP.max))
+                lin("zn" + x, "V", zn, ap("xs", 512 * h + 3, 512 * h + 512, 4), 1.0, -256.0)
+            tile = "P:y" + x
+            if cfg["ymode"][2 * t + h] == "A":
+                lst = []
+                for j in range(4):
+                    for q in range(4):
+                        m = ap("yp", 144 * j + 12 - 4 * q, 144 * j + 140 - 4 * q)
+                        o = ps(tile, 32 * j, 32 * j + 32)
+                        lst += [(o, m, ap("es", n * h + q, n * h + n, 4)), (o, m, ap("sv", n * h + q, n * h + n, 4))]
+                mms("y" + x, lst)
+                lin("yl" + x, "S", c("yl", h), ps(tile, 0, n), 4096.0, -2040.0, True)
+                for j in range(4):
+                    src = ind(ap("mt"), c("yl", h, 1, 32 * j, 32 * j + 32))
+                    if j == 0:
+                        lin("ya0" + x, "V", c("ya", h, 4), src)
+                    else:
+                        tt("ya%d" % j + x, c("ya", h, 4), src, c("ya", h, 4), OP.max)
+                op("yn" + x, "V", ("scan", c("yn", h, 16, 0, 512), ap("rx"), c("ya", h, 4), 0.0, OP.mult, OP.max))
+                best = ap("yn", 2048 * h + 3, 2048 * h + 512, 4)
+            else:
+                mms("y" + x, [(ps(tile, 0, n), ap("ib"), es), (ps(tile, 0, n), ap("ib"), sv)])
+                lin("yl" + x, "S", c("yl", h), ps(tile, 0, n), 4096.0, -2040.0, True)
+                for j in range(GP):
+                    part = (h, 16, 16 * gl * j, 16 * gl * (j + 1))
+                    lin("yb%d" % j + x, "S", c("yw", *part), ind(ap("mt"), c("yl", h, 1, gl * j, gl * j + gl)))
+                    op("yn%d" % j + x, "V", ("scan", c("yn", *part), ap("r16", 0, 16 * gl), c("yw", *part), 0.0, OP.mult, OP.max))
+                best = ap("yn", 2048 * h + 15, 2048 * h + 2048, 16)
+            if last:
+                lin("sn" + x, "S", c("ysf", h), best)
+                op("o.s%d" % h, "Y", ("dma", ap("ys", n * h, n * h + n), c("ysf", h)))
+                op("o.z%d" % h, "Y", ("dma", ap("yz", n * h, n * h + n), zn))
+            else:
+                sn = ap("ss", 256 * t + n * h, 256 * t + n * h + n)
+                lin("sn" + x, "V", sn, best)
+                zd = 384 * (2 * t + 2 + h)
+                op("ms" + x, "G", ("send", ap("su", 256 * t + 256 + n * h, 256 * t + 256 + n * h + n), sn, 4 * t + 2 * h))
+                op("mz" + x, "G", ("send", ap("zq", zd + 256, zd + 384), zn, 4 * t + 2 * h + 1))
+            tt("si" + x, c("si", h), ind(xw(h), ap("l2", 24 * h + 8, 24 * h + 16)), zn, OP.add)
+            ts("sj" + x, c("sj", h), c("si", h), 1, None, OP.logical_shift_right)
+            op("xc" + x, "V", ("copy", ind(ap("xt"), ap("l2", 24 * h, 24 * h + 8)), c("sj", h)))
+            if last:
+                for j in range(2):
+                    lin("ch%d%d" % (h, j), "S", c("gw", h, 16, 1024 * j, 1024 * j + 1024), c("ct", h, 16, 1024 * j, 1024 * j + 1024), 1.0, -2048.0)
+                    mms("yc%d%d" % (h, j), [(ps("P:yc", 0, 256), ap("mi", 128 * m, 128 * m + 128), ap("gw", 256 * m, 256 * m + 256))
+                                            for m in range(8 * h + 4 * j, 8 * h + 4 * j + 4)], h + j == 0, h + j == 2)
+                tile = "P:yx%d" % h
+                mms("yx%d" % h, [(ps(tile, 0, n), ap("mi", 128 * m, 128 * m + 128), ap("xt", 256 * m + n * h, 256 * m + n * h + n))
+                                 for m in range(16)])
+                lin("oyx%d" % h, "S", c("oyx", h), ps(tile, 0, n))
+                op("o.x%d" % h, "Y", ("dma", ap("yx", n * h, n * h + n), c("oyx", h)))
+        if not last:
+            tt("a.%d" % t, ap("acol", 2, 3), ap("acol", 0, 1), ap("acol", 1, 2), OP.add)
+            op("da.%d" % t, "S", ("act", ap("da"), ap("i32"), AF.Identity, -15856.0, ap("acol", 2, 3), None))
+    lin("oyc", "S", ap("oyc"), ps("P:yc", 0, 256), 1.0, 2048.0 * 136)
+    op("o.c", "A", ("dma", ap("yc"), ap("oyc")))
+    return ops
+
+
+def touches(o):
+    rd, wr = [], []
+
+    def add(lst, a):
+        cs = cols(a)
+        lst.append((a[1], int(cs.min()), int(cs.max())))
+
+    for cl in o["calls"]:
+        outs = [1, 6] if cl[0] == "act" else [1]
+        for i, a in enumerate(cl):
+            if not isap(a):
+                continue
+            if a[0] == "ind":
+                add(wr if i in outs else rd, a[1])
+                add(rd, a[2])
+            else:
+                add(wr if i in outs else rd, a)
+    return rd, wr
+
+
+def edges(ops):
+    seen = {}
+    preds = []
+    for i, o in enumerate(ops):
+        rd, wr = touches(o)
+        p = {}
+        for lst, w in ((rd, False), (wr, True)):
+            for (b, lo, hi) in lst:
+                if b in DRAM:
+                    continue
+                psum = b.startswith("P:")
+                for (j, lo2, hi2, w2) in seen.get(b, []):
+                    if j == i:
+                        continue
+                    if psum:
+                        p[j] = max(p.get(j, 0), 1 if (w2 and not w) else 0)
+                    elif (w or w2) and lo <= hi2 and lo2 <= hi:
+                        p[j] = 1
+        for lst, w in ((rd, False), (wr, True)):
+            for (b, lo, hi) in lst:
+                seen.setdefault(b, []).append((i, lo, hi, w))
+        preds.append(p)
+        o["tiles"] = sorted(set(b for (b, _l, _h) in rd + wr if b.startswith("P:")))
+    return preds
+
+
+def queue_of(e):
+    return "S" if e == "A" else e
+
+
+def timing(ops, K):
+    busy, after = [], []
+    for o in ops:
+        tm = sum(call_cost(cl, K) for cl in o["calls"])
+        if o["eng"] == "P":
+            tm += K["pfix"]
+        busy.append(tm)
+        after.append(K["dlat"] if o["eng"] in "YA" else K["slat"] if o["calls"][0][0] == "send" else 0.0)
+    return busy, after
+
+
+def lag(ops, j, i, kind, K):
+    if ops[j]["eng"] == ops[i]["eng"] and ops[j]["eng"] in "VSPG" and ops[j]["calls"][0][0] != "send":
+        return K["own"] if kind and ops[j]["eng"] != "P" else 0.0
+    return K["wake"]
+
+
+def schedule(ops, preds, cfg, K, bonus=None):
+    N = len(ops)
+    busy, after = timing(ops, K)
+    succ = [[] for _ in range(N)]
+    for i in range(N):
+        for j in preds[i]:
+            succ[j].append(i)
+    level = [0.0] * N
+    for i in range(N - 1, -1, -1):
+        level[i] = busy[i] + after[i] + max([level[s] + lag(ops, i, s, preds[s][i], K) for s in succ[i]] + [0.0])
+    r = cfg["seed"] * 7919 + 13
+    prio = []
+    for i in range(N):
+        r = (r * 1103515245 + 12345) % 2147483648
+        prio.append(level[i] + cfg["jit"] * (r / 2147483648.0 - 0.5) + (bonus[i] if bonus else 0.0))
+    users = {}
+    for i in range(N):
+        for b in ops[i]["tiles"]:
+            users.setdefault(b, []).append(i)
+    left = [len(p) for p in preds]
+    ready = [i for i in range(N) if left[i] == 0]
+    end = [0.0] * N
+    done = [False] * N
+    free = {}
+    holder = [None] * 8
+    bank = {}
+    order = []
+    rt = {i: 0.0 for i in ready}
+    while ready:
+        cand = []
+        for i in ready:
+            e = ops[i]["eng"]
+            st = max(rt[i], free.get("Y" if e == "A" else e, 0.0), free.get("S", 0.0) if e == "A" else 0.0)
+            bk = None
+            new = [b for b in ops[i]["tiles"] if b not in bank]
+            if new:
+                pool = range(cfg["xbanks"]) if new[0][2] == "x" else range(cfg["xbanks"], 8)
+                opts = []
+                for b in pool:
+                    hd = holder[b]
+                    if hd is None:
+                        opts.append((0.0, b))
+                    elif all(done[u] for u in users[hd]):
+                        opts.append((max(end[u] for u in users[hd]) + K["wake"], b))
+                if not opts:
+                    continue
+                tb, bk = min(opts)
+                st = max(st, tb)
+            cand.append((st, i, bk))
+        if not cand:
+            return None
+        t0, i0, _b = min(cand)
+        q = queue_of(ops[i0]["eng"])
+        st, i, bk = max([cd for cd in cand if queue_of(ops[cd[1]]["eng"]) == q and cd[0] <= t0 + cfg["delta"]], key=lambda cd: prio[cd[1]])
+        if bk is not None:
+            b = [b for b in ops[i]["tiles"] if b not in bank][0]
+            bank[b] = bk
+            holder[bk] = b
+        e = ops[i]["eng"]
+        if e == "A":
+            free["S"] = st + 60.0
+            free["Y"] = st + busy[i]
+        else:
+            free[e] = st + busy[i]
+        end[i] = st + busy[i] + after[i]
+        done[i] = True
+        order.append(i)
+        ready.remove(i)
+        for s in succ[i]:
+            left[s] -= 1
+            if left[s] == 0:
+                ready.append(s)
+                rt[s] = max(end[j] + lag(ops, j, s, kd, K) for j, kd in preds[s].items())
+    return order, bank, max(end)
+
+
+def with_banks(ops, preds, order, bank):
+    full = [dict(p) for p in preds]
+    users, lastt = {}, {}
+    for i in range(len(ops)):
+        for b in ops[i]["tiles"]:
+            users.setdefault(b, []).append(i)
+    for i in order:
+        for b in ops[i]["tiles"]:
+            if users[b][0] == i:
+                if bank[b] in lastt:
+                    for u in users[lastt[bank[b]]]:
+                        full[i][u] = max(full[i].get(u, 0), 0)
+                lastt[bank[b]] = b
+    return full
+
+
+def waits(ops, full, order):
+    pos, cnt = {}, {}
+    for i in order:
+        o = ops[i]
+        own = o["eng"] in "YA" or o["calls"][0][0] == "send"
+        key = ("own", i) if own else o["eng"]
+        cnt[key] = cnt.get(key, 0) + 1
+        pos[i] = (key, cnt[key])
+    known = {}
+    clock = {}
+    need = {}
+    for i in order:
+        q = queue_of(ops[i]["eng"])
+        kn = known.setdefault(q, {})
+        want = {}
+        for j, kind in full[i].items():
+            key, p = pos[j]
+            if key == ops[i]["eng"] and (kind == 0 or key == "P"):
+                continue
+            if kn.get(key, 0) < p and want.get(key, (0, 0))[0] < p:
+                want[key] = (p, j)
+        lst = []
+        for key, (p, j) in sorted(want.items(), key=lambda kv: -order.index(kv[1][1])):
+            if kn.get(key, 0) >= p:
+                continue
+            lst.append(j)
+            for k2, p2 in clock[j].items():
+                if kn.get(k2, 0) < p2:
+                    kn[k2] = p2
+        need[i] = lst
+        key, p = pos[i]
+        if ops[i]["calls"][0][0] == "send":
+            clock[i] = {key: p}
+        else:
+            clock[i] = dict(kn)
+            clock[i][key] = p
+    return need
+
+
+PLAN = {}
+
+
+def plan():
+    if not PLAN:
+        ops = build(CFG)
+        preds = edges(ops)
+        if CFG["order"]:
+            o = CFG["order"]
+            order = [int(o[i:i + 2], 36) for i in range(0, len(o), 2)]
+            bank = banks(ops, order)
+        else:
+            order, bank, _t = schedule(ops, preds, CFG, COST)
+        PLAN["p"] = (ops, order, bank, waits(ops, with_banks(ops, preds, order, bank), order))
+    return PLAN["p"]
+
+
+def banks(ops, order):
+    lastuse = {}
+    for p, i in enumerate(order):
+        for b in ops[i]["tiles"]:
+            lastuse[b] = p
+    until, bank = [-1] * 8, {}
+    for p, i in enumerate(order):
+        for b in ops[i]["tiles"]:
+            if b not in bank:
+                k = until.index(min(until))
+                assert until[k] < p
+                bank[b] = k
+                until[k] = lastuse[b]
+    return bank
+
+
+def lanes_engines(topo, src, dst):
+    e = topo.engines(src, dst)
+    return e[::max(1, len(e) // CFG["ne"])]
+
+
+def rank_program(g, core, T, topo):
+    rank = T.rank_of(core)
+    if rank is None:
+        return
+    ops, order, bank, need = plan()
+    nxt = T.cores[(rank + 1) % len(T.cores)]
+    prv = T.cores[(rank - 1) % len(T.cores)]
+    assert topo.may_write(core, nxt)
+    out_eng = lanes_engines(topo, core, nxt)
+    rid, pid = topo.addr(nxt)[0:2]
+    Q = {"V": g.vector, "S": g.scalar, "P": g.tensor, "G": g, "Y": g.sync, "A": g.scalar}
+
+    def R(a):
+        if not isap(a):
+            return a
+        if a[0] == "ind":
+            return R(a[1]).indirect(R(a[2]))
+        return T["ps%d" % bank[a[1]] if a[1].startswith("P:") else a[1]][a[2]]
+
+    waited = set(j for i in order for j in need[i])
+    sig, cnt, nd, sent = {}, {}, [0], [0]
+    for i in order:
+        o = ops[i]
+        q = Q[o["eng"]]
+        for j in need[i]:
+            q.wait_ge(T.sem[sig[j][0]], sig[j][1])
+        ins = None
+        for cl in o["calls"]:
+            k, a = cl[0], [R(v) for v in cl[1:]]
+            if k == "mm":
+                ins = q.matmul(*a)
+            elif k == "ts":
+                ins = q.tensor_scalar(*a[:5]) if a[5] is None else q.tensor_scalar(*a)
+            elif k == "tt":
+                ins = q.tensor_tensor(*a)
+            elif k == "copy":
+                ins = q.tensor_copy(*a)
+            elif k == "memset":
+                ins = q.memset(*a)
+            elif k == "scan":
+                ins = q.tensor_tensor_scan(*a)
+            elif k == "act":
+                ins = q.activation(a[0], a[1], a[2], bias=a[3], scale=a[4], accum_out=a[5])
+            elif k == "iota":
+                if shape_of(cl[1][1])[1] == I32:
+                    ins = q.iota(*a)
+                else:
+                    ins = q.iota(*a, allow_small_or_imprecise_dtypes=True)
+            elif k == "sel":
+                ins = q.affine_select(*a)
+            elif k == "dma":
+                ins = q.dma_start(a[0], a[1])
+            elif k == "send":
+                sem = "ar%d" % a[2]
+                q.remote_dma(a[0], a[1], T.sem[sem], T.sem.left, pid, rid, sum(1 << e for e in out_eng))
+                sig[i] = (sem, len(lanes_engines(topo, prv, core)))
+                sent[0] += len(out_eng)
+        if o["eng"] in "YA":
+            sig[i] = ("d%d" % nd[0], 16)
+            nd[0] += 1
+            ins.then_inc(T.sem[sig[i][0]], 16)
+        elif i in waited and i not in sig:
+            cnt[o["eng"]] = cnt.get(o["eng"], 0) + 1
+            sig[i] = (o["eng"], cnt[o["eng"]])
+            ins.then_inc(T.sem[o["eng"]], 1)
+    g.wait_ge(T.sem.left, sent[0])
+    for i in order:
+        if ops[i]["eng"] in "YA" and i not in waited:
+            g.sync.wait_ge(T.sem[sig[i][0]], 16)

@@ -4,28 +4,30 @@ from concourse.mybir import AluOpType as OP, ActivationFunctionType as AF
 LEVELS, H, n = 4, 2, 128
 F32, BF, F16, I32, U16 = "float32", "bfloat16", "float16", "int32", "uint16"
 SB = {
-    "mt": (4104, I32), "ct": (4096, I32), "xt": (4096, BF), "s0i": (256, I32),
-    "gw": (4096, F16), "xw": (4128, BF), "es": (256, F16), "u1": (256, F32), "eq": (2048, F16),
-    "p1": (256, F32), "p2": (256, I32), "hh": (256, I32), "h16": (256, U16), "hi": (256, BF),
-    "ti": (256, I32), "bb": (256, BF), "ind": (768, BF), "sg": (256, BF), "sr": (256, BF), "sv": (256, BF),
-    "t1": (256, BF), "rr": (2 * 1920, F32), "ft": (256, F32), "fv": (256, I32), "l2": (48, U16),
-    "ui": (16, I32), "uj": (16, I32), "lc": (16, U16), "xa": (1024, F16), "xs": (1024, F16), "yl": (256, U16),
-    "ya": (1024, F32), "yw": (4096, F32), "yn": (4096, F32), "si": (256, I32), "sj": (256, I32),
-    "zq": (8 * 384, BF), "su": (1024, U16), "zs": (1024, BF), "ss": (768, U16), "ysf": (256, F32),
-    "junk": (256, BF), "acol": (8, F32), "da": (128, F16), "oyx": (256, F32), "oyc": (256, F32),
-    "ones": (256, BF), "idf": (128, F32), "ib": (128, BF), "i32": (128, BF), "i4k": (128, BF), "ob": (128, BF),
-    "o2k": (128, BF), "lo": (128, BF), "l4k": (128, BF), "b1": (128, BF), "qa": (128, BF), "fi": (128, BF),
-    "wd": (2304, BF), "o1": (144, BF), "bw": (144, BF), "dm": (1024, BF), "ad": (1024, F16), "rs": (2048, BF),
-    "yp": (576, BF), "mi": (2048, BF), "sm": (96, F32), "raw": (64, F32), "pm": (16, F32), "r0": (1024, BF),
-    "tie": (80, F32), "im": (128, BF), "pos": (128, F16), "xl": (256, U16), "xm": (4096, BF), "xn": (4096, BF), "qi": (4, I32), "qf": (16, F32), "dd": (8, F32),
-    "tau": (24, F32), "a16": (8, F32), "rx": (512, BF), "r16": (1024, BF),
+    "cr": (4096, I32), "ct": (4096, I32), "cf": (4096, F32), "mt": (4104, I32), "xt": (4096, BF),
+    "s0i": (256, I32), "z0b": (256, BF),
+    "gw": (4096, F16), "xw": (4096, BF), "es": (256, F16), "eq": (2048, F16), "p1": (256, F32), "p2": (256, I32),
+    "hh": (256, I32), "h16": (256, U16), "hf": (256, F16), "s4": (256, F16), "tf": (768, F16), "sg": (256, BF),
+    "sr": (256, BF), "tr": (256, BF), "rr": (2 * 1920, F32), "ft": (256, F32), "fv": (256, F32),
+    "ua": (512, U16), "ub": (1024, U16), "uc": (2048, U16), "ud": (4096, F16),
+    "ui": (64, I32), "l2": (64, U16), "xs": (4096, F16), "xd": (4096, BF), "yl": (256, U16), "ya": (4096, F16),
+    "yn": (4096, F16), "si": (256, I32), "sj": (256, I32), "zq": (4 * 768, F16), "su": (1024, U16), "zs": (768, F16),
+    "zo": (256, BF), "ss": (768, U16), "ysf": (256, F32), "junk": (16, BF), "acol": (8, F32), "av": (128, F16),
+    "oyx": (256, F32), "oyc": (256, F32),
+    "ones": (256, BF), "twos": (32, BF), "idf": (128, F32), "ib": (128, BF), "i4k": (128, BF), "n4k": (128, BF),
+    "i33": (128, BF), "n256": (128, BF), "ob": (128, BF), "o2k": (128, BF), "lo": (128, BF), "up": (128, BF),
+    "u4k": (128, BF), "tm": (128, BF), "qa": (128, BF), "s3m": (128, BF), "wd": (2304, BF), "w0": (1152, BF),
+    "o1": (144, BF), "bw": (144, BF), "dm": (1024, BF), "ad": (1024, F16), "rs": (2048, BF), "r0": (1024, BF),
+    "mi": (2048, BF), "rx": (1024, BF), "stat": (64, F32), "a16": (32, F32),
+    "raw": (80, F32), "cy": (64, F32), "sm": (80, F32), "pm": (16, F32), "tie": (48, F32), "m4": (16, F32),
+    "im": (128, BF), "qi": (8, I32), "qf": (24, F32), "dd": (8, F32), "tau": (24, F32),
 }
 SCRATCH = {k: ("sbuf", [128, v[0]], v[1]) for k, v in SB.items()}
-SCRATCH["stat"] = ("sbuf", [128, 6, 8], BF)
 SCRATCH["zz"] = ("sbuf", [128, 8, 32], BF)
-SCRATCH["st"] = ("sbuf", [128, 6, 8, 16], F16)
+SCRATCH["st"] = ("sbuf", [128, 5, 8, 16], BF)
+FLAT = 6
 for _b in range(8):
-    SCRATCH["ps%d" % _b] = ("psum", [128, 32, 16], F32)
+    SCRATCH["ps%d" % _b] = ("psum", [128, 512] if _b < FLAT else [128, 32, 16], F32)
 SEMAPHORES = (["V", "S", "P", "G", "left"] + ["ar%d" % i for i in range(12)] + ["d%d" % i for i in range(24)])
 DRAM = {"x0": (4096, BF), "cm": (4096, I32), "s0": (256, I32), "z0": (256, BF),
         "yx": (256, F32), "yc": (256, F32), "ys": (256, F32), "yz": (256, BF)}
@@ -33,21 +35,15 @@ ALL = slice(None)
 COLS = {}
 
 CFG = {
-    "ymode": "AAAAAAAB",
-    "xmode": "AAAAAAAB",
-    "eng": {},
-    "seed": 1, "jit": 0.0, "delta": 200.0, "xbanks": 2, "ne": 8, "gp": 4, "order": None,
+    "blocks": (0, 1280, 2560, 3584, 4096),
+    "parts": {"gc": (4, 4), "gx": (4, 4), "ya": (4, 4)},
+    "sort": "FF",
+    "via": (),
+    "ne": 8,
 }
-CFG.update({
-    "ymode": "ABABABAB", "xmode": "BABABABA",
-    "order": "030j241l1p0s0v0x0w251z1t1w1q1u1r0t0p280y1k040q1j2x39200k0u0r1s0o1n0l050m100n171m311o2e2f1v29181x1a21191y06161f221c2608231b1i0f0e2z2a09000z1g024t272b0g1e2d3l1d1h2c0a14013u2q133a2u2g2h120d0b0c113o4u3p3n3q150i0h4n3r3s3t3x3z403y074m3v4q4p4o41373w3b4243442w2i2s2v2j4r4s474w464y4z4x324v3c3e4a2y48492p35502k51332l524b2m2t532n554c4d4f4e3d3f583g4g564h4i594j4k57453j5a4l3h5b5c36543k30345d5e3m5l6v5m2r6w765f3i77615g73785h5n625i5j5k79746x6l657u7m7v71727a7k636667687w697b5o6z5p6m6n6p5q826a7y6q7c6s7d6y6t70837z7x5t5r5s6b6c5u6e5v5w7e5x6d5y806f75816g6h6i2o5z606r6j6k6u7j7l7n8c7o7p7g84648f6o7f7q8j8d7r7h8a8e8g8h7s8k8b7i857t8i8m8o878l8n8p8q9d8r889c9b869e8s8t899f8v9g9h9n8x9i9l8w9j8y8z908u9m9o9192949p93959k96979q9r389s9v9t98999a9uaqbk9w9xaabl9yarbm9za0a1abacada3bvbsbobqa2aebnafbwbxa4a5a6bpa7bra8a9baauagavbbahbcasaibybzajawakaxayc0cjckbeazclbfbgc1alamb0anb3aob1b2apcpb4b5b6b7cnc9btbubhc2b8cbcrcmbibjcscqcoc3b9cactatcdc4c8ccbdd2ced1c5cfd3d4cgc6chczcid5d6cuc7d8d7dbd9cvddcwd0dadcdee2e0e3dfe1dgcxe4dhdicydke5e6dldmdne7eaecdodpedebeee8dqdrdte9dsdudvefegeheidwdxekejdydzg9ezdjemffengagbeleofgf0epeqeserfhgfgkgcgleteugmf1f2evewexggeyfjgnf3gdfzh8h9gof4fkhcg0gyf5gphgflgqf8h0g1g3g4g6f7f6gzfmfnhafog5f9fah2fsh1g7hdgrfphbhhfbfqhehfgsfrg2fch4ftfufvh3gehifdfwfehjfifxfyg8gxh5ghhrhqgihogjh6guhshugthth7hkhvisgvhwipiqi2hlgwi0i3i1irithxhpiuhyi4iviziwhmhzixhni5i6i7j1j0j2iyiaj3i9j4icidj5j6ibj9iej8ifjcjbjai8igihiiijikiliminiojdjojpk4kwjejqjfjhjgj7kxjijrjsjjk5k6jtl2jul0l7jkl8jll4jxjmkyjnjyknk7kolulskpl9k8l1kzl3jvjwlaltl5lvm2kqkrk9jzkakbk0ksl6k1ktlwlyk2kckglhkulilxk3lzkdkhlbm0kekim3lgkfmam6kjkkklljkvm1lomfkmmglrm4mhmmm7lplcmnldmelqlembm5molflkmilmlllnmjmkm8mlm9mcmpmqmd",
-})
-CFG.update({
-    "order": "0s0u1p0j28031w040t0x1z1x0w1t0v0k1q0y392x1n171l180p1y1r0q2e0o10112420190e1u2113050r3a0n291s1v2a1a0z1j1m2w1e08311k2f220f06262z2q231d1c25092d2b14000m0102162u0g1i1h271f2c0a0b0l1o3u2g0d0c2h4t1b1g123o3p0h0i3n3r153q4n3v3s3t4u3z4m073x4p404o2p4q3l3y2i2y3w412j3b4243442v3d4r374s4y4w464z4x323e4v472s354a3c495051482k2l4b33453f523g4c2m2n532t4d4f4e554g583m564h4i4j594k573j5a36544l6v6w3h5b30765l5c3k736z5d5e5f5g2r345h777461785i5m5j3i5k5n656l797u66677k6x717262635o5p645q6m6n6y707a7v6p7b7w7m6q7c5u5r68695s6a6s5t5v7d5w7y6t757x6b6c6e7e5x6f827z835y6d6g807f5z6h816i606u6o6j6k7j8a847l6r8d8e8f8j7n7o8c7p7q857g7r8g8k2o8b8h8i8m7h7s7t869b9c7i8o878n8p888l898q8r8s8t9e9d9f9g8v9i8x8w9h9l9j8y9n8z909k9m9o919p9293949q9r9s8u95969v979t98999aaqbk9u9w9xblaaab38ar9ybm9za0acadbsa1a2a3aeafbva4a5bobqbwa6bna7bxbpbrbtajasa8a9ahauavcjbybackawagakalbzaxc0ayc1buaiamanbbbcbeclcmazb1aob3c9b0b4b5apb2cpcnb6bfb7b8atcabgbdc2bhcrcbbicsbjcqcoc3ctb9c8d1d4cdc4ccc5d2c6cucfd3ced5d6d7c7cgczchd8d9dbddd0dadcdecicwe3dfe0cve1e2dgcxdhdicye4dke5e6ecdldmdneadoe7e8dpebeddqdrdtdse9eeefegehdjdudvejeidwdxdyekdzffg9enelemgaeogbezgkfgfhgfepeqeresgletgcf0euf1evgmf2ewexggeyfjfzh8gngoh9f3gdfkflh0gyf4g0g1fmfnhagpgzfofpf7frf6gqg3f5g4grfsh2f8fthghbgef9h1hhhefqg6hffahcfbfufifvhdfcg7g2fdfwfxgsh4hifeh3g5g8fyhjgxghhqgihrh5gjhshuguh6gvgth7hthkipiqhvishwhoi0gwhli2i3i1hmirithxiuhphyhzi4ivhni5iziwi6j0j1j2ixi7ibj3iyiaj4j5j6j9i9idicieifj8igjcihiiijjbjaikilj7iminjdioi8jojpjejfjhjgkwkxk4k5k6jqjijrjsjtl7kyjul8jjjkl2kzjll9jxjmjwjyjnjvk7knk8lsjzlukol4kpltl0l3lal5l1k9lvl6kakbkckqkrlwksk0k1kdlylxm2m3lgk2lhktkflzlikekgkhkim0k3maljm6kjlokkklkum1kvmflbkmmglrmhm4lclplkllmemmm5ldlqlmmimnlem7mblfmomkm8m9lnmcmjmlmpmqmd",
-    "engs": "000180eb04704b6c010040f3882ac02ce71582b02448130255f9088142588a13c493c18028e48412",
-})
-COST = {"f": 1.2, "cyc": 0.83, "pe": 0.417, "r": 1.56, "sc": 3.8, "vfix": 60.0, "sfix": 75.0, "pfix": 30.0,
-        "wake": 100.0, "own": 60.0, "bw": 220.0, "dlat": 1800.0, "send": 1000.0, "slat": 3000.0, "tt2": 2.0}
+ROUND = 'p2.1 r0.1@0 -k.lo r1.1@0 -k.q2 k.st1 -k.wd0 -k.qf -k.dm5 -k.dm7 -k.wd2 tf2.0 s1.0 oyx sg.0 s2.0 hh.1 h16.1 gx0.1 k.n4k hf.1 sr.0 tf0.0@0 tf2.0@0 tf1.0@0 s3.0 s1.0@0 sv.0 p2.1@0 k.n256 hh.1@0 h16.1@0 gx0.1@0 sg.0@0 s2.0@0 k.rt1 hf.1@0 sr.0@0 -k.twos -k.t1 -k.fb0 gx1.1@0 gx1.1 gx2.1 y.0 x10.0 q.0@3 s3.0@0 y.0@3 -k.fb1 -k.b1 -k.t2 -k.b0 -k.t3 -k.b2 gx3.1 sv.0@0 -k.t4 yl.0 yl.0@3 ya1.0@3 bn0.1 q.0@0 t.0@3 y.0@0 gx2.1@0 tr.0@3 ya2.0@3 t.0 ya0.0 gx3.1@0 bn0.1@0 t.0@0 x10.0@0 ya3.0 ya1.0 yl.0@0 bn1.1 xs10.0 tr.0 s4.1 q.0 +o.x.0 k.0 bn1.1@0 x01.0 ya0.0@3 k.st20 tr.0@0 tf2.1 tf0.1 x01.0@3 x11.0@0 x10.0@3 -m0 -k.dq -k.ad5 -k.fb2 -k.ad4 -k.ad7 -k.ad8 tf1.1 q1.0@3 ra.0 rb.0 ya2.0 q1.0@0 ya0.0@0 ya2.0@0 ya1.0@0 -k.k32 -k.pm0 -k.s3 -k.rb -k.pm1 -k.b3 s4.1@0 k.st21 x01.0@0 tf1.1@0 tf2.1@0 tf0.1@0 s1.1@0 xs01.0@3 xs10.0@0 xs01.0@0 xs01.0 s1.1 k.0@0 ya3.0@0 yn1.0 k.0@3 sg.1 sg.1@0 s2.1@0 sr.1@0 x11.0 x00.0@0 -c0 -k.ad6 -k.ad3 -k.i33 yn1.0@0 +o.x.1 wp.0 -m1 s3.1@0 rc.0 --ld.c0 --ld.z s2.1 x00.0@3 ra.0@3 rb.0@3 --ld.s ra.0@0 sv.1@0 sr.1 x00.0 s3.1 rb.0@0 rc.0@0 rd.0@0 rf.0@0 re.0@0 yn0.0@0 fa.0@0 y.1@0 yl.1@0 re.0 rd.0 fa.0 q.1@0 t.1@0 xs10.0@3 +oyc xb.0@0 x11.1@0 yn0.0@3 sv.1 rc.0@3 y.1 q1.1@0 tr.1@0 t.1 fb.0 q.1 ya0.1@0 ya2.1@0 sn.0@0 ya1.1@0 k.1@0 xb.1@0 l@0 fb.0@0 ui@0 xs11.0@0 yn0.1@0 ra.1@0 -k.s3m -k.s4 -av0 rb.1@0 ya3.1@0 yn1.1@0 uk@0 rf.0 tr.1 k.1 x11.1 fc.0 fd.0 yn0.0 q1.0 yl.1 sn.0 -k.ad2 -k.ad1 ya2.1 ya0.1 wq.0 ya1.1 re.0@3 rf.0@3 ya3.1 q1.1 +o.c yn0.1 l xb.0 sn.1@0 ra.1 rc.1@0 rd.1@0 ya3.0@3 rb.1 xb.0@3 x11.0@3 q.1@3 t.1@3 y.1@3 rd.0@3 tr.1@3 q1.1@3 x11.1@3 yl.1@3 fa.0@3 xs11.0@3 re.1@0 rf.1@0 yn1.0@3 xs11.1@3 rc.1 rd.1 re.1 -su0 -k.dq2 fc.0@0 fd.0@0 rf.1 ft.0 ya3.1@3 l@3 k.1@3 fa.1@0 fb.1@0 fc.1@0 fd.1@0 ra.1@3 ya0.1@3 rb.1@3 ui fa.1 fb.1 fb.0@3 x01.1@3 xs00.0@3 ya1.1@3 ns fc.0@3 fd.0@3 --ld.c1 zn.0@3 ui@3 -k.tie x00.1@3 ft.0@3 yn1.1 fc.1 xs00.0 fd.1 ft.0@0 fe.0 ft.1@0 ms.0 xb.1 ms.0@0 sn.1 uj@3 uk@3 fe.0@0 yn0.1@3 fe.1@0 fv.0@0 rc.1@3 ya2.1@3 rd.1@3 xs00.0@0 xs11.1 xs11.0 ft.1 fv.0 -cf0 -k.ti2 x10.1@0 ms.1@0 uk fe.1 av re.1@3 rf.1@3 sn.0@3 fe.0@3 wp.1 xb.1@3 fa.1@3 uj@0 xs01.1@3 fv.1@0 yn1.1@3 -c1 ns@0 fb.1@3 uj x01.1@0 fv.0@3 -k.s5 -k.qa -z0 -k.s7 -k.s61 -k.s60 zn.0@0 fc.1@3 fd.1@3 x00.1@0 lc@3 xs00.1@3 si.0 lc@0 -k.s8 -k.i4k -c2 -k.s62 -k.st0 mz.0@0 zn.0 ms.1 fv.1 lc -k.dm4 cs.0@3 x01.1 cs.0 -k.dm6 -k.wd1 av@0 -k.dm3 cs.1 xs01.1 wq.1 xs11.1@0 cs.0@0 x00.1 cs.1@0 -gc1.0 xs10.1@0 -gc0.0 x10.1 xs00.1 xs01.1@0 xs00.1@0 -gc2.0 xs10.1 -d10.0 mz.0 k.mi00 k.mi10 -c3 sn.1@3 --ld.c2 -cf3 -k.sx0 -k.bw -cf1 -k.ti1 -k.dm1 -k.up -cf2 -k.dm2 -k.dm8 -k.ti3 -k.ra ch1.0 --k.m4 --k.q ft.1@3 -gc3.0 -gc0.0@0 -d11.0 fe.1@3 fv.1@3 -k.rs2 zn.1@0 -gc1.0@0 -gc3.0@0 si@0 cs.1@3 x10.1@3 xs10.1@3 --ld.c3 sj.0 zn.1@3 -d10.0@0 si.1 dl.0 o.s.0 -gc2.1@0 sj.1 mz.1@0 -u.0 ch0.0 -gc2.0@0 -d11.0@0 ch0.1 -gc1.1 -gc0.1 -es.0@0 o.z.0 -gc2.1 -gc3.1 zn.1 si dm.0 dl.1 -es.0 mz.1 --k.ones --k.rs0 --k.q1 k.mi01 k.mi11 k.mi02 k.mi12 k.mi03 -gc0.1@0 -u.1@0 -m3 -gc1.1@0 -u.0@0 -k.ti4 -gc3.1@0 sj@0 -p1.0@0 -k.sx1 -k.ti5 -df0.0@0 k.mi13 --ld.x -eq0.0@0 yc0.0 -df0.0 -df1.0 -k.ti6 -df1.0@0 -eq1.0@0 -k.rx0 o.s.1 o.z.1 -k.rs1 yc1.0 ch1.1 -r0.0@0 sj -p1.0 -eq0.0 -eq1.0 -d10.1 -r0.0 -r1.0 yc0.1 yc1.1 -d11.1 xc -yx xc@0 -r1.0@0 -p2.0@0 -es.1 -df0.1 -d10.1@0 -k.ti7 -d11.1@0 -df1.1 -p2.0 --k.ob1 --k.s0 --k.im --k.dd -k.rt2 -hh.0 --k.ob2 -h16.0 -gx0.0 -m2 -gx1.0 --k.q3 --k.s1 -gx2.0 -hh.0@0 --k.q4 -k.tm0 -h16.0@0 -k.sx2 --k.a16 -gx3.0 -u.1 -eq0.1 -k.sx3 -gx1.0@0 -k.tm1 -es.1@0 -k.rx1 -gx3.0@0 -df1.1@0 -df0.1@0 -eq1.1 -bn0.0 -k.qa1 -gx0.0@0 --k.s2 --k.w --k.o2k --k.o10 -bn1.0 --k.ib -bn0.0@0 -m4 -r0.1 -p1.1@0 -gx2.0@0 -k.sx4 -eq0.1@0 -k.sx5 -bn1.0@0 -s4.0@0 --k.zz -eq1.1@0 -r1.1 -k.sx6 -hf.0@0 -k.idf -k.sx7 -hf.0 -k.ti8 -k.u4k -p1.1 dn.0 --k.o1 dm.1 dn.1 -s4.0 -tf1.0 -tf0.0'
+ENG = 'av:S cf3:V ch0.0:G ch0.1:S ch1.1:S es.0:V es.1@0:V ft.0@3:V fv.1@3:V gc1.0@0:V gc2.0:V gc2.0@0:S gc2.1@0:V gc3.0@0:V gx0.0:V gx0.1:V gx2.0:V gx2.1@0:V gx3.1:V gx3.1@0:S k.i4k:V k.n256:V k.s3m:V k.sx0:V k.sx1:V k.sx2:V k.sx4:V m1:S m2:S m3:S m4:S ra.0:V ra.0@0:S ra.0@3:S rb.0:V rb.0@0:S rb.0@3:S s4.1:V sg.0:S sg.1:S sj.0:S sn.0@3:S sn.1@3:S sr.1@0:V tf2.0:S tf2.0@0:V tr.0:V tr.0@3:S tr.1@0:V tr.1@3:V ui:S ui@0:V ui@3:V wq.0:S wq.1:S ya0.1:V ya0.1@3:S ya1.0@0:V ya1.0@3:V ya1.1:V ya1.1@0:S ya2.0:V ya2.0@0:S ya2.0@3:S ya2.1@0:V ya3.0@3:V yl.0:V yl.1:V yl.1@3:S'
+CFG["eng"] = dict(v.split(":") for v in ENG.split())
 
 
 def ap(name, a=None, b=None, s=None):
@@ -86,53 +82,17 @@ def isap(a):
     return isinstance(a, tuple) and len(a) == 3 and a[0] in ("ap", "ind")
 
 
-def two(a):
-    return shape_of(a[1])[1] in (BF, F16, U16)
-
-
-def call_cost(c, K):
-    k = c[0]
-    cy = K["cyc"] * K["f"]
-    if k == "mm":
-        N, M = len(cols(c[3])), len(cols(c[2]))
-        return max(min(64, M), N) * (4 if shape_of(c[2][1])[1] == F32 else 1) * K["pe"] * K["f"]
-    if k == "iota":
-        return 130 + 2 * len(cols(c[1])) * cy
-    if k == "sel":
-        return 170 + 2 * len(cols(c[1])) * cy
-    if k == "dma":
-        return 128 * len(cols(c[1])) * (2 if two(c[1]) else 4) / K["bw"]
-    if k == "send":
-        return K["send"]
-    fix = K["sfix"] if k == "act" else K["vfix"]
-    aps = [a for a in c[1:] if isap(a)]
-    if c[1][0] == "ind":
-        return fix + 16 * len(cols(c[1][2])) * K["sc"] * cy
-    m = len(cols(c[1]))
-    if any(a[0] == "ind" for a in aps):
-        return fix + m * K["r"] * cy
-    if k == "act":
-        return fix + max(64, m) * cy
-    if k == "tt":
-        both = not (c[2][1].startswith("P:") or c[3][1].startswith("P:"))
-        return fix + max(64, m * (K["tt2"] if both else 1)) * cy
-    wide = [a for a in aps if len(cols(a)) > 1]
-    return fix + max(64, m * (0.5 if all(two(a) for a in wide) else 1)) * cy
-
-
 def build(cfg):
     ops = []
     cfg["free"] = {}
+    lev = [0]
 
     def op(name, eng, *calls):
-        ops.append({"name": name, "eng": eng, "calls": list(calls)})
+        ops.append({"key": name, "t": lev[0], "eng": eng, "calls": list(calls)})
 
     def eng(name, dflt):
         cfg["free"][name] = dflt
-        if cfg.get("engs"):
-            k = len(cfg["free"]) - 1
-            return "V" if int(cfg["engs"][k // 4], 16) >> (3 - k % 4) & 1 else "S"
-        return cfg["eng"].get(name, dflt)
+        return cfg["eng"].get("%s@%d" % (name, lev[0]), cfg["eng"].get(name, dflt))
 
     def lin(name, dflt, out, in_, scale=1.0, bias=0.0, relu=False):
         if eng(name, dflt) == "S":
@@ -140,9 +100,9 @@ def build(cfg):
         elif relu and shape_of(out[1])[1] != U16:
             assert scale == 1.0
             op(name, "V", ("ts", out, in_, bias, 0.0, OP.add, OP.max))
-        elif scale == 1.0 and not isap(bias) and bias == 0.0:
+        elif not isap(scale) and scale == 1.0 and not isap(bias) and bias == 0.0:
             op(name, "V", ("copy", out, in_))
-        elif scale == 1.0:
+        elif not isap(scale) and scale == 1.0:
             op(name, "V", ("ts", out, in_, bias, None, OP.add, None))
         else:
             op(name, "V", ("ts", out, in_, scale, bias, OP.mult, OP.add))
@@ -162,24 +122,8 @@ def build(cfg):
     def col(j):
         return ap("qf", j, j + 1)
 
-    op("ld.s", "A", ("dma", ap("s0i"), ap("s0")))
-    for h in range(H):
-        op("ld.z%d" % h, "A", ("dma", ap("zq", 384 * h + 256, 384 * h + 384), ap("z0", n * h, n * h + n)))
-    NC = cfg.get("nc", 4)
-    w = 4096 // NC
-    for j in range(NC):
-        op("ld.c%d" % j, "Y", ("dma", ap("mt", 8 + w * j, 8 + w * j + w), ap("cm", w * j, w * j + w)))
-    op("ld.x", "Y", ("dma", ap("xt"), ap("x0")))
-    for j in range(NC):
-        ts("c%d" % j, ap("ct", w * j, w * j + w), ap("mt", 8 + w * j, 8 + w * j + w), 4095, None, OP.bitwise_and)
-    for h in range(H):
-        lin("su0.%d" % h, "S", ap("su", n * h, n * h + n), ap("s0i", n * h, n * h + n))
-    fill("m0", ap("mt", 0, 8), 0)
-    for j in range(NC):
-        ts("m%d" % (j + 1), ap("mt", 8 + w * j, 8 + w * j + w), ap("mt", 8 + w * j, 8 + w * j + w), 12, None, OP.logical_shift_right)
-
-    def sel(name, out, in_, pat, cmp, base, ch):
-        op(name, "G", ("sel", out, in_, pat, cmp, 0.0, base, ch))
+    def sel(name, out, in_, pat, cmp, base, ch, v=0.0):
+        op(name, "G", ("sel", out, in_, pat, cmp, v, base, ch))
 
     def diag(name, out, in_, v):
         op(name, "G", ("sel", out, in_, [[-1, 128]], OP.not_equal, v, 0, 1))
@@ -187,23 +131,54 @@ def build(cfg):
     def iota(name, out, pat, base, ch):
         op(name, "G", ("iota", out, pat, base, ch))
 
+    def gather(name, h, out, win, lst, p0, p1):
+        m = cfg["parts"][name][h]
+        w = n // m
+        for p in range(p0 * m // 4, p1 * m // 4):
+            a = lst[2][1].start + w * p
+            lin("%s%d.%d" % (name, p, h), "S", c(out, h, 16, 16 * w * p, 16 * w * p + 16 * w), ind(win, ap(lst[1], a, a + w)))
+
+    def st(j):
+        return ("ap", "st", (ALL, j, ALL, ALL))
+
+    def c(name, h, m=1, a=0, b=None, s=None):
+        return ap(name, m * n * h + a, m * n * h + (m * n if b is None else b), s)
+
+    bl = cfg["blocks"]
+    op("ld.s", "A", ("dma", ap("s0i"), ap("s0")))
+    op("ld.z", "A", ("dma", ap("z0b"), ap("z0")))
+    for j in range(len(bl) - 1):
+        op("ld.c%d" % j, "Y", ("dma", ap("cr", bl[j], bl[j + 1]), ap("cm", bl[j], bl[j + 1])))
+    op("ld.x", "Y", ("dma", ap("xt"), ap("x0")))
+    for j in range(len(bl) - 1):
+        ts("c%d" % j, ap("ct", bl[j], bl[j + 1]), ap("cr", bl[j], bl[j + 1]), 4095, None, OP.bitwise_and)
+        lin("cf%d" % j, "S", ap("cf", bl[j], bl[j + 1]), ap("ct", bl[j], bl[j + 1]), 1.0, -2048.0)
+    lin("su0", "S", ap("su", 0, 256), ap("s0i"))
+    lin("z0", "S", ap("zq", 512, 768), ap("z0b"))
+    fill("av0", ap("av"), -20352.0)
+    fill("m0", ap("mt", 0, 8), -2047)
+    for j in range(len(bl) - 1):
+        lin("m%d" % (j + 1), "V", ap("mt", 8 + bl[j], 8 + bl[j + 1]), ap("cr", bl[j], bl[j + 1]), 1.0 / 4096, -2047.5 + 1.0 / 8192)
+
     fill("k.ones", ap("ones"), 1.0)
-    fill("k.wd0", ap("wd"), 1.0 / 4096)
+    fill("k.twos", ap("twos"), 2.0)
+    fill("k.wd0", ap("w0"), 1.0)
     for j in range(2):
-        sel("k.wd%d" % (j + 1), ap("wd", 1152 * j, 1152 * j + 1152), ap("wd", 1152 * j, 1152 * j + 1152),
+        sel("k.wd%d" % (j + 1), ap("wd", 1152 * j, 1152 * j + 1152), ap("w0"),
             [[-1, 8], [-16, 9], [1000, 16]], OP.is_equal, -15000 - 8 * j, 1)
     sel("k.ib", ap("ib"), ap("ones", 0, 128), [[-1, 128]], OP.is_equal, 0, 1)
     sel("k.zz", ap3("zz", ALL, ALL), ap("ones"), [[-16, 8], [0, 2], [-1, 16]], OP.is_equal, 0, 1)
     sel("k.ob1", ap("ob"), ap("ones", 0, 128), [[-16, 8], [0, 16]], OP.is_ge, 0, 1)
     sel("k.ob2", ap("ob"), ap("ob"), [[16, 8], [0, 16]], OP.is_ge, 15, -1)
     sel("k.lo", ap("lo"), ap("ob"), [[1, 128]], OP.is_gt, 0, -1)
+    sel("k.up", ap("up"), ap("ob"), [[-1, 128]], OP.is_gt, 0, 1)
     iota("k.q", ap("qi", 0, 1), [[0, 1]], 0, 1)
     iota("k.dd", ap("dd"), [[1, 8]], 1, 0)
     iota("k.im", ap("im"), [[1, 128]], 0, 0)
     ts("k.q1", ap("qi", 1, 2), ap("qi", 0, 1), 15, None, OP.bitwise_and)
     ts("k.q2", ap("qi", 2, 3), ap("qi", 0, 1), 2, 3, OP.logical_shift_right, OP.bitwise_and)
     ts("k.q3", ap("qi", 3, 4), ap("qi", 0, 1), 3, None, OP.bitwise_and)
-    lin("k.qf", "V", ap("qf", 0, 4), ap("qi"))
+    lin("k.qf", "V", ap("qf", 0, 4), ap("qi", 0, 4))
     for d in range(1, 9):
         diag("k.dm%d" % d, ap("dm", 128 * d - 128, 128 * d), ap3("zz", ALL, slice(d, d + 16)), -1.0)
     ts("k.t1", ap("tau", 0, 8), ap("dd"), col(1), 15.0, OP.add, OP.is_le)
@@ -213,265 +188,255 @@ def build(cfg):
     for d in range(1, 9):
         ts("k.ad%d" % d, ap("ad", 128 * d - 128, 128 * d), ap("im"), ap("tau", 15 + d, 16 + d),
            col(4) if d == 8 else 19616.0, OP.is_equal, OP.mult)
-    lin("k.o2k", "S", ap("o2k"), ap("ob"), 2048.0)
-    lin("k.da", "S", ap("da"), ap("ones", 0, 128), -15856.0)
+    for name, src, v in (("o2k", "ob", 2048.0), ("i33", "ib", 33.0), ("i4k", "ib", 4096.0), ("n4k", "ib", -4096.0),
+                         ("n256", "ib", -256.0), ("u4k", "up", 4096.0), ("idf", "ib", 1.0), ("qa", "lo", -4096.0)):
+        lin("k." + name, "S", ap(name), ap(src), v)
+    diag("k.qa1", ap("qa"), ap("qa"), 4096.0)
+    tt("k.tm0", ap("tm"), ap("up"), ap("lo"), OP.subtract)
+    diag("k.tm1", ap("tm"), ap("tm"), 32.0)
     fill("k.o10", ap("o1"), 0.0)
     lin("k.o1", "S", ap("o1", 15, 143, 16), ap("ob", 0, 128, 16))
-    lin("k.w", "S", col(5), col(0), 0.5, 0.25)
-    op("k.bw", "S", ("act", ap("bw"), ap("o1"), AF.Identity, 0.0, col(5), None))
-    fill("k.s0", ap("raw"), 0.0)
-    for j in range(4):
-        fill("k.sa%d" % j, ap("raw", 17 * j, 16 * j + 16, 4), 16.0)
-        fill("k.sb%d" % j, ap("raw", 20 * j, 20 * j + 4), -16.0)
-        fill("k.sc%d" % j, ap("raw", 21 * j, 21 * j + 1), 4.0)
-    tt("k.sd", ap("sm", 32, 80), ap("raw", 16, 64), ap("raw", 0, 48), OP.subtract)
-    tt("k.se", ap("sm", 0, 32), ap("sm", 48, 80), ap("sm", 32, 64), OP.subtract)
+    ts("k.q4", ap("qi", 4, 5), ap("qi", 0, 1), 1, None, OP.bitwise_and)
+    lin("k.w", "S", col(5), ap("qi", 4, 5), -0.5, 0.25)
+    lin("k.bw", "S", ap("bw"), ap("o1"), col(5))
+    sel("k.s0", ap("raw", 16, 80), ap("ones", 0, 64), [[-1, 4], [0, 4], [1, 4]], OP.is_equal, 0, 0)
+    sel("k.s1", ap("raw", 16, 80), ap("raw", 16, 80), [[-1, 4], [1, 4], [0, 4]], OP.not_equal, 0, 0, -1.0)
+    sel("k.s2", ap("raw", 16, 80), ap("raw", 16, 80), [[-6, 4], [1, 4], [5, 4]], OP.not_equal, 0, 0, 1.0)
+    lin("k.s3", "S", ap("raw", 0, 16), ap("raw", 64, 80))
+    tt("k.s4", ap("cy"), ap("raw", 16, 80), ap("raw", 0, 64), OP.subtract)
+    lin("k.s5", "S", ap("sm", 0, 16), ap("cy", 16, 32), 4.0)
+    for j, c0 in enumerate((0, 48, 32)):
+        tt("k.s6%d" % j, ap("sm", 16 + 16 * j, 32 + 16 * j), ap("cy", c0, c0 + 16), ap("cy", 16, 32), OP.subtract)
     iota("k.tie", ap("tie", 0, 16), [[-2, 4], [2, 4]], -1, 0)
-    lin("k.tie2", "S", ap("tie", 0, 16), ap("tie", 0, 16), 1.0 / 32)
-    lin("k.sh", "S", ap("tie", 16, 32), ap("raw", 0, 16), 0.25)
-    tt("k.sf", ap("sm", 48, 64), ap("tie", 0, 16), ap("tie", 16, 32), OP.add)
-    iota("k.m4", ap("tie", 64, 80), [[1, 4], [0, 4]], 0, 0)
+    lin("k.ti1", "S", ap("tie", 0, 16), ap("tie", 0, 16), 1.0 / 8)
+    lin("k.ti2", "S", ap("tie", 16, 32), ap("raw", 16, 32), 16.0)
+    lin("k.ti3", "S", ap("tie", 32, 48), ap("cy", 16, 32), 98304.0)
+    tt("k.ti4", ap("tie", 0, 16), ap("tie", 0, 16), ap("tie", 16, 32), OP.add)
+    tt("k.ti5", ap("tie", 0, 16), ap("tie", 0, 16), ap("tie", 32, 48), OP.add)
+    ts("k.ti6", ap("tie", 16, 32), ap("im", 0, 16), col(1), None, OP.is_equal)
+    tt("k.ti7", ap("tie", 0, 16), ap("tie", 0, 16), ap("tie", 16, 32), OP.mult)
+    op("k.ti8", "S", ("act", ap("tie", 32, 48), ap("tie", 0, 16), AF.Identity, 0.0, 1.0, col(12)))
+    iota("k.m4", ap("m4"), [[1, 4], [0, 4]], 0, 0)
     tt("k.dq", col(6), col(2), col(3), OP.is_equal)
     lin("k.dq2", "S", col(11), col(6), 4.0, 1.0)
-    ts("k.s2a", ap("sm", 64, 80), ap("tie", 64, 80), col(2), col(11), OP.is_equal, OP.mult)
-    ts("k.s2b", ap("sm", 64, 80), ap("sm", 64, 80), col(6), None, OP.subtract)
-    ts("k.s3", ap("sm", 80, 96), ap("ones", 0, 16), col(2), 1.0 / 16, OP.mult, OP.mult)
+    ts("k.s7", ap("sm", 64, 80), ap("m4"), col(2), col(11), OP.is_equal, OP.mult)
+    ts("k.s8", ap("sm", 64, 80), ap("sm", 64, 80), col(6), None, OP.subtract)
     lin("k.pm0", "S", ap("pm", 0, 16, 2), ap("ob", 0, 128, 16), -1.0)
     lin("k.pm1", "S", ap("pm", 1, 16, 2), ap("ob", 0, 128, 16))
     for j in range(8):
-        op("k.sx%d" % j, "S", ("act", ("ap", "st", (ALL, ALL, j, ALL)), ap("sm"), AF.Identity, 0.0, ap("pm", 2 * j + 1, 2 * j + 2), None))
-    lin("k.i32", "S", ap("i32"), ap("ib"), 32.0)
-    lin("k.i4k", "S", ap("i4k"), ap("ib"), 4096.0)
-    lin("k.l4k", "S", ap("l4k"), ap("lo"), 4096.0)
-    lin("k.idf", "S", ap("idf"), ap("ib"))
-    lin("k.qa0", "S", ap("qa"), ap("lo"), -4096.0)
-    diag("k.qa1", ap("qa"), ap("qa"), 4096.0)
-    lin("k.b10", "S", ap("b1"), ap("lo"), -2.0)
-    diag("k.b11", ap("b1"), ap("b1"), -32.0)
-    lin("k.fi", "S", ap("fi"), ap("o1", 15, 143), 4096.0)
-    lin("k.k16", "S", col(7), col(1), 1.0, -16.0)
-    ts("k.fb0", col(8), col(1), 0.0, 524288.0, OP.is_equal, OP.mult)
-    lin("k.fb1", "S", col(9), col(1), 4096.0, -61440.0)
-    tt("k.fb2", col(10), col(8), col(9), OP.add)
-    lin("k.a16", "S", ap("a16"), ap("dd"), 16.0, -16.0)
-    fill("k.st0", ap3("stat", ALL, ALL), 0.0)
+        lin("k.sx%d" % j, "S", ("ap", "st", (ALL, ALL, j, ALL)), ap("sm"), ap("pm", 2 * j + 1, 2 * j + 2))
+    ts("k.b0", col(17), col(3), 0.0, col(2), OP.is_equal, OP.mult)
+    ts("k.b1", col(18), col(3), 1.0, -6144.0, OP.is_equal, OP.mult)
+    tt("k.b2", col(19), col(17), col(18), OP.add)
+    lin("k.b3", "S", col(20), col(19), 0.25)
+    lin("k.s3m", "S", ap("s3m"), ap("ob"), col(20))
+    lin("k.k32", "S", col(7), col(1), 1.0, -32.0)
+    if "F" in cfg["sort"]:
+        ts("k.fb0", col(8), col(1), 0.0, 524288.0, OP.is_equal, OP.mult)
+        lin("k.fb1", "S", col(9), col(1), 4096.0, -63488.0)
+        tt("k.fb2", col(10), col(8), col(9), OP.add)
+        lin("k.ra", "S", col(21), col(1), 4096.0, -2048.0)
+        lin("k.rb", "S", col(22), col(1), 4096.0, -6144.0)
+    if "U" in cfg["sort"]:
+        lin("k.ua", "S", col(23), col(1), 4096.0, 2048.0)
+        lin("k.ub", "S", col(14), col(1), 4096.0, -30720.0)
+    iota("k.a16", ap("a16"), [[16, 32]], 0, 0)
+    fill("k.st0", ap("stat", 0, 32), 32768.0)
+    ts("k.st1", ap("stat", 48, 64), ap("a16", 0, 16), col(1), None, OP.add)
     for h in range(H):
-        ts("k.st1%d" % h, ap3("stat", 3 * h, ALL), ap("a16"), col(1), 128.0 * h, OP.add, OP.add)
-        ts("k.st2%d" % h, ap3("stat", 3 * h + 1, ALL), ap("a16"), col(1), 16.0, OP.add, OP.mult)
-    if "B" in cfg["xmode"]:
-        for h in range(H):
-            fill("k.xz%d" % h, ap("xw", 2064 * h, 2064 * h + 16), 0.0)
-        lin("k.pos0", "S", col(12), col(1), 1.0, -1024.0)
-        lin("k.pos1", "S", ap("pos"), ap("im"), 16.0, col(12))
+        ts("k.st2%d" % h, ap("stat", 32 + 8 * h, 40 + 8 * h), ap("stat", 48, 56), 16.0, None, OP.mult)
     fill("k.rs0", ap("r0"), 256.0)
     for j in range(2):
         sel("k.rs%d" % (j + 1), ap("rs", 1024 * j, 1024 * j + 1024), ap("r0"), [[-1, 8], [-16, 8], [0, 16]], OP.is_equal, -8 * j, 1)
-    lin("k.yp0", "S", ap("yp"), ap("r0", 0, 576), 1.0 / 256)
-    sel("k.yp1", ap("yp"), ap("yp"), [[-4, 4], [-16, 9], [-1, 16]], OP.is_equal, 12, 1)
-    sel("k.yp2", ap("yp"), ap("yp"), [[0, 36], [1, 16]], OP.is_ge, -12, 0)
-    lin("k.rx0", "S", ap("rx"), ap("r0", 0, 512), 1.0 / 256)
-    lin("k.rx1", "S", ap("rx", 0, 512, 4), ap("r0", 0, 128), 0.0)
-    if "B" in cfg["ymode"] + cfg["xmode"]:
-        lin("k.r160", "S", ap("r16"), ap("r0"), 1.0 / 256)
-        lin("k.r161", "S", ap("r16", 0, 1024, 16), ap("r0", 0, 64), 0.0)
-    iota("k.mi0", ap("mi"), [[1, 16], [0, 128]], 1, 0)
-    sel("k.mi1", ap("mi"), ap("mi"), [[0, 16], [-1, 128]], OP.is_equal, 0, 1)
-
-    GP = cfg["gp"]
-    gl = n // GP
-
-    def xw(h, a=0, b=2048, s=None):
-        return ap("xw", 2064 * h + 16 + a, 2064 * h + 16 + b, s)
-
-    def st(j):
-        return ("ap", "st", (ALL, j, ALL, ALL))
-
-    def c(name, h, m=1, a=0, b=None):
-        return ap(name, m * n * h + a, m * n * h + (m * n if b is None else b))
+        sel("k.rt%d" % (j + 1), ap("rs", 1024 * j, 896 * j + 1024), ap("rs", 1024 * j, 896 * j + 1024),
+            [[-1, 8 - j], [-16, 8], [0, 16]], OP.not_equal, -8 * j - 1, 1, -256.0)
+    fill("k.rx0", ap("rx"), 0.0)
+    fill("k.rx1", ap("rx", 0, 1024, 16), -4096.0)
+    for j in range(4):
+        iota("k.mi0%d" % j, ap("mi", 512 * j, 512 * j + 512), [[1, 4], [0, 128]], 1 + 4 * j, 0)
+        sel("k.mi1%d" % j, ap("mi", 512 * j, 512 * j + 512), ap("mi", 512 * j, 512 * j + 512), [[0, 4], [-1, 128]], OP.is_equal, 0, 1)
 
     for t in range(LEVELS):
+        lev[0] = t
         last = t == LEVELS - 1
+
+        def zq(h, j, tt_=t):
+            a = 768 * tt_ + n * (2 * j + h)
+            return ap("zq", a, a + n)
+
+        def tile(name, h):
+            return "P:%s%d.%d" % (name, t, h)
+
         for h in range(H):
-            x = ".%d%d" % (t, h)
-            zb = 384 * (2 * t + h)
-            z = ap("zq", zb + 256, zb + 384)
-            for j in range(GP):
-                lin("g1" + x + str(j), "S", c("gw", h, 16, 16 * gl * j, 16 * gl * (j + 1)),
-                    ind(ap("ct"), ap("su", 256 * t + n * h + gl * j, 256 * t + n * h + gl * j + gl)), 1.0, -2048.0)
-            pe = ps("P:e" + x, 0, n)
+            x = ".%d" % h
+            z = zq(h, 2)
             for j in range(2):
-                mms("d1" + x + str(j), [(ps("P:e" + x, 64 * j, 64 * j + 64), ap("wd", 144 * ((k + t) & 15) + 15 - k, 144 * ((k + t) & 15) + 143 - k),
-                                         ap("gw", 2048 * h + 1024 * j + k, 2048 * h + 1024 * j + 1024, 16)) for k in range(16)], j == 0, j == 1)
-            lin("es" + x, "V", c("es", h), pe)
-            pu = ps("P:u" + x, 0, n)
+                gather("gc", h, "gw", ap("cf"), ap("su", 256 * t + n * h, 256 * t + n * h + n), 2 * j, 2 * j + 2)
+                mms("d1%d" % j + x, [(ps(tile("e", h), 64 * j, 64 * j + 64),
+                                      ap("wd", 144 * ((k + t) & 15) + 15 - k, 144 * ((k + t) & 15) + 143 - k),
+                                      c("gw", h, 16, 1024 * j + k, 1024 * j + 1024, 16)) for k in range(16)], j == 0, j == 1)
+            es = c("es", h)
+            lin("es" + x, "S", es, ps(tile("e", h), 0, n))
+            pu = ps(tile("u", h), 0, n)
             mms("u" + x, [(pu, ap("ob"), z)])
-            lin("u1" + x, "S", c("u1", h), pu, 4096.0, 33.0 * 4096)
-            tt("p1" + x, c("p1", h), pe, c("u1", h), OP.mult)
+            tt("p1" + x, c("p1", h), pu, es, OP.mult)
             for j in range(2):
-                tile = "P:d%d" % j + x
-                mms("df%d" % j + x, [(ps(tile, n * i, n * i + n), ap("dm", 512 * j + 128 * i, 512 * j + 128 * i + 128), c("es", h))
-                                     for i in range(4)])
-                ts("eq%d" % j + x, c("eq", h, 8, 512 * j, 512 * j + 512), ps(tile, 0, 512), 0.0, None, OP.is_equal)
-            pr = ps("P:r" + x, 0, n)
-            mms("r" + x, [(pr, ap("da"), ap("ones", 0, n)), (pr, ap("o2k"), z)] +
-                [(pr, ap("ad", 128 * d, 128 * d + 128), c("eq", h, 8, n * d, n * d + n)) for d in range(8)])
+                tl = tile("d%d" % j, h)
+                mms("df%d" % j + x, [(ps(tl, n * i, n * i + n), ap("dm", 512 * j + 128 * i, 512 * j + 128 * i + 128), es) for i in range(4)])
+                ts("eq%d" % j + x, c("eq", h, 8, 512 * j, 512 * j + 512), ps(tl, 0, 512), 0.0, None, OP.is_equal)
+            pr = ps(tile("r", h), 0, n)
+            pairs = [(pr, ap("ad", 128 * d, 128 * d + 128), c("eq", h, 8, n * d, n * d + n)) for d in range(8)]
+            mms("r0" + x, [(pr, ap("ob"), ap("av")), (pr, ap("o2k"), z), (pr, ap("i33"), es)] + pairs[:4], True, False)
+            mms("r1" + x, pairs[4:], False, True)
             tt("p2" + x, c("p2", h), pr, c("p1", h), OP.add)
             ts("hh" + x, c("hh", h), c("p2", h), 5, 4095, OP.arith_shift_right, OP.bitwise_and)
             lin("h16" + x, "V", c("h16", h), c("hh", h))
-            lin("hi" + x, "V", c("hi", h), c("hh", h), 1.0, 36736.5)
-            for j in range(GP):
-                lin("g2" + x + str(j), "S", xw(h, 16 * gl * j, 16 * gl * (j + 1)),
-                    ind(ap("xt"), c("h16", h, 1, gl * j, gl * j + gl)))
-            pb = ps("P:b" + x, 0, n)
+            lin("hf" + x, "S", c("hf", h), c("hh", h), 1.0, -2048.0)
+            pb = ps(tile("b", h), 0, n)
             for j in range(2):
-                mms("bn" + x + str(j), [(ps("P:b" + x, 64 * j, 64 * j + 64), ap("bw", 15 - k, 143 - k),
-                                         xw(h, 1024 * j + k, 1024 * j + 1024, 16)) for k in range(16)], j == 0, j == 1)
-            ts("ti" + x, c("ti", h), pb, -0.375, None, OP.add)
-            tt("bb" + x, c("bb", h), pb, c("ti", h), OP.subtract)
-            for j in range(2):
-                lin("i%d" % j + x, "V", c("ind", h, 2, n * j, n * j + n), c("bb", h), 1.0, -0.25 * (j + 1), True)
-            p1 = ps("P:s1" + x, 0, n)
-            mms("s1" + x, [(p1, st(3), ap("ones", 0, n)), (p1, st(2), c("bb", h))] +
-                [(p1, st(j), c("ind", h, 2, n * j, n * j + n)) for j in range(2)])
+                gather("gx", h, "xw", ap("xt"), c("h16", h), 2 * j, 2 * j + 2)
+                mms("bn%d" % j + x, [(ps(tile("b", h), 64 * j, 64 * j + 64), ap("bw", 15 - k, 143 - k),
+                                      c("xw", h, 16, 1024 * j + k, 1024 * j + 1024, 16)) for k in range(16)], j == 0, j == 1)
+            s4 = c("s4", h)
+            lin("s4" + x, "S", s4, pb)
+            for j in range(3):
+                lin("tf%d" % j + x, "V", c("tf", h, 3, n * j, n * j + n), s4, 1.0, 1535.625 + 0.25 * j)
+            p1 = ps(tile("s1", h), 0, n)
+            mms("s1" + x, [(p1, st(0), s4)] + [(p1, st(j + 1), c("tf", h, 3, n * j, n * j + n)) for j in range(3)])
             signs = eng("sg" + x, "V") == "S"
             if signs:
-                op("sg" + x, "S", ("act", c("sg", h), p1, AF.Sign, 0.0, 1.0, None))
+                op("sg" + x, "S", ("act", c("sg", h), p1, AF.Sign, col(12), 1.0, None))
             else:
-                ts("sg" + x, c("sg", h), p1, 0.0, None, OP.is_gt)
-            p2 = ps("P:s2" + x, 0, n)
+                ts("sg" + x, c("sg", h), p1, col(12), 0.0, OP.add, OP.is_gt)
+            p2 = ps(tile("s2", h), 0, n)
             mms("s2" + x, [(p2, st(4), c("sg", h))])
-            if eng("sr" + x, "V") == "S":
+            if eng("sr" + x, "S") == "S":
                 op("sr" + x, "S", ("act", c("sr", h), p2, AF.Relu, -1.0 if signs else -3.0, 0.5 if signs else 1.0, None))
             else:
                 ts("sr" + x, c("sr", h), p2, 4.0, None, OP.is_equal)
-            p3 = ps("P:s3" + x, 0, n)
-            mms("s3" + x, [(p3, st(5), c("sr", h))])
-            tt("sv" + x, c("sv", h), p3, c("bb", h), OP.is_equal)
+            p3 = ps(tile("s3", h), 0, n)
+            mms("s3" + x, [(p3, ap("ib"), c("tf", h, 3, 0, n)), (p3, ap("s3m"), c("sr", h))])
+            tt("sv" + x, zq(h, 1), p3, s4, OP.is_equal)
         for h in range(H):
-            x = ".%d%d" % (t, h)
-            zb = 384 * (2 * t + h)
-            sv, es = c("sv", h), c("es", h)
-            pt = ps("P:t" + x, 0, n)
-            mms("t" + x, [(pt, ap("ob"), sv), (pt, ap("b1"), sv)])
-            lin("t1" + x, "S", c("t1", h), pt, 1.0, col(1), True)
-            pk = ps("P:k" + x, 0, n)
-            mms("k" + x, [(pk, ap("l4k"), sv), (pk, ap("i4k"), es), (pk, ap("i4k"), c("t1", h))])
-            lin("ra" + x, "S", c("rr", h, 15, 0, n), pk, 1.0, -2048.0, True)
-            lin("rb" + x, "S", c("rr", h, 15, n, 2 * n), pk, 1.0, -6144.0, True)
-            lin("rc" + x, "S", c("rr", h, 15, 2 * n, 4 * n), c("rr", h, 15, 0, 2 * n), 1.0, -8192.0, True)
-            lin("rd" + x, "S", c("rr", h, 15, 4 * n, 8 * n), c("rr", h, 15, 0, 4 * n), 1.0, -16384.0, True)
-            lin("re" + x, "S", c("rr", h, 15, 8 * n, 12 * n), c("rr", h, 15, 0, 4 * n), 1.0, -32768.0, True)
-            lin("rf" + x, "S", c("rr", h, 15, 12 * n, 15 * n), c("rr", h, 15, 0, 3 * n), 1.0, -49152.0, True)
-            tile = "P:f" + x
-            fm = [(ps(tile, 0, n), es, ap("fi"))] + [(ap3(tile, slice(0, 8), slice(p - 1, p + 1)), c("rr", h, 15, n * p - n, n * p), ap("pm"))
-                                                    for p in range(1, 16)]
-            mms("fa" + x, fm[:5], True, False)
-            mms("fb" + x, fm[5:9], False, False)
-            mms("fc" + x, fm[9:13], False, False)
-            mms("fd" + x, fm[13:], False, True)
-            lin("ft" + x, "S", c("ft", h), ps(tile, 0, n))
-            pf = ps("P:g" + x, 0, n)
-            mms("fe" + x, [(pf, c("ft", h), ap("idf"))])
-            lin("fv" + x, "S", c("fv", h), pf, 1.0, col(10))
-            tile = "P:q" + x
-            mms("q" + x, [(ps(tile, 0, n), ap("ib"), c("hi", h)), (ps(tile, 0, n), ap("qa"), sv), (ps(tile, n, 2 * n), ap("qa"), sv)] +
-                ([] if last else [(ps(tile, 2 * n, 3 * n), ap("ob"), sv)]))
-            lin("q1" + x, "S", ap("zq", zb, zb + n), ps(tile, 0, n), 1.0, -40960.0, True)
-            op("q2" + x, "S", ("act", ap("zq", zb + n, zb + 2 * n), ps(tile, n, 2 * n), AF.Relu, col(7), 1.0 / 256, None))
-            if not last:
-                op("ns" + x, "S", ("act", c("junk", h), ps(tile, 2 * n, 3 * n), AF.Relu, 2.0, -1.0, ap("acol", h, h + 1)))
-            if h == 1:
-                tile = "P:l" + x
-                pl = ap3(tile, slice(0, 6), slice(0, 8))
-                mms("l" + x, [(pl, ap("ib"), ap3("stat", ALL, ALL))] +
-                    [(pl, ap("o1", 15 - b, 143 - b), ap("zq", zb - 384 + b, zb + 384, 16)) for b in range(16)])
-                lin("ui" + x, "V", ap("ui"), ap3(tile, slice(2, 6, 3), slice(0, 8)))
-                lin("l2" + x, "V", ap("l2"), pl)
-                ts("uj" + x, ap("uj"), ap("ui"), 15, None, OP.bitwise_and)
-                tt("lc" + x, ap("lc"), ap("uj"), ap3("stat", slice(1, 6, 3), ALL), OP.add)
-        for h in range(H):
-            x = ".%d%d" % (t, h)
-            sv, es = c("sv", h), c("es", h)
-            op("cs" + x, "V", ("copy", ind(c("ct", h, 16), ap("lc", 8 * h, 8 * h + 8)), c("fv", h)))
-            zn = ap("zs", 256 * t + n * h, 256 * t + n * h + n)
-            if cfg["xmode"][2 * t + h] == "B":
-                tile = "P:x" + x
-                mms("x" + x, [(ps(tile, 0, n), ap("ib"), ap("pos")), (ps(tile, 0, n), ap("i4k"), sv)])
-                lin("xl" + x, "S", c("xl", h), ps(tile, 0, n), 1.0, -3056.0, True)
-                for j in range(GP):
-                    part = (h, 16, 16 * gl * j, 16 * gl * (j + 1))
-                    lin("xb%d" % j + x, "S", c("xm", *part), ind(xw(h, -16), c("xl", h, 1, gl * j, gl * j + gl)))
-                    op("xn%d" % j + x, "V", ("scan", c("xn", *part), ap("r16", 0, 16 * gl), c("xm", *part), 0.0, OP.mult, OP.max))
-                lin("zn" + x, "V", zn, ap("xn", 2048 * h + 15, 2048 * h + 2048, 16))
-            for j in range(4 if cfg["xmode"][2 * t + h] == "A" else 0):
-                tile = "P:x%d" % j + x
-                lst = []
-                for s in range(4):
-                    k = 4 * j + s
-                    o = ap3(tile, ALL, slice(s, 16, 4))
-                    lst += [(o, ap("ib"), xw(h, k, 2048, 16)), (o, ap("rs", 128 * k, 128 * k + 128), sv)]
-                mms("x%d" % j + x, lst)
-                if j == 0:
-                    lin("xa0" + x, "S", c("xa", h, 4), ps(tile, 0, 512))
-                else:
-                    tt("xa%d" % j + x, c("xa", h, 4), ps(tile, 0, 512), c("xa", h, 4), OP.max)
-            if cfg["xmode"][2 * t + h] == "A":
-                op("xs" + x, "V", ("scan", c("xs", h, 4), ap("rx"), c("xa", h, 4), 0.0, OP.mult, OP.max))
-                lin("zn" + x, "V", zn, ap("xs", 512 * h + 3, 512 * h + 512, 4), 1.0, -256.0)
-            tile = "P:y" + x
-            if cfg["ymode"][2 * t + h] == "A":
-                lst = []
-                for j in range(4):
-                    for q in range(4):
-                        m = ap("yp", 144 * j + 12 - 4 * q, 144 * j + 140 - 4 * q)
-                        o = ps(tile, 32 * j, 32 * j + 32)
-                        lst += [(o, m, ap("es", n * h + q, n * h + n, 4)), (o, m, ap("sv", n * h + q, n * h + n, 4))]
-                mms("y" + x, lst)
-                lin("yl" + x, "S", c("yl", h), ps(tile, 0, n), 4096.0, -2040.0, True)
-                for j in range(4):
-                    src = ind(ap("mt"), c("yl", h, 1, 32 * j, 32 * j + 32))
-                    if j == 0:
-                        lin("ya0" + x, "V", c("ya", h, 4), src)
-                    else:
-                        tt("ya%d" % j + x, c("ya", h, 4), src, c("ya", h, 4), OP.max)
-                op("yn" + x, "V", ("scan", c("yn", h, 16, 0, 512), ap("rx"), c("ya", h, 4), 0.0, OP.mult, OP.max))
-                best = ap("yn", 2048 * h + 3, 2048 * h + 512, 4)
+            x = ".%d" % h
+            sv, es = zq(h, 1), c("es", h)
+            pt = ps(tile("t", h), 0, n)
+            mms("t" + x, [(pt, ap("tm"), sv)])
+            lin("tr" + x, "S", c("tr", h), pt, 1.0, col(7), True)
+            pk = ps(tile("k", h), 0, n)
+            mms("k" + x, [(pk, ap("u4k"), sv), (pk, ap("ib"), es), (pk, ap("n4k"), c("tr", h))])
+            pf = ps(tile("g", h), 0, n)
+            if cfg["sort"][h] == "F":
+                lin("ra" + x, "S", c("rr", h, 15, 0, n), pk, 1.0, col(21), True)
+                lin("rb" + x, "S", c("rr", h, 15, n, 2 * n), pk, 1.0, col(22), True)
+                lin("rc" + x, "S", c("rr", h, 15, 2 * n, 4 * n), c("rr", h, 15, 0, 2 * n), 1.0, -8192.0, True)
+                lin("rd" + x, "S", c("rr", h, 15, 4 * n, 8 * n), c("rr", h, 15, 0, 4 * n), 1.0, -16384.0, True)
+                lin("re" + x, "S", c("rr", h, 15, 8 * n, 12 * n), c("rr", h, 15, 0, 4 * n), 1.0, -32768.0, True)
+                lin("rf" + x, "S", c("rr", h, 15, 12 * n, 15 * n), c("rr", h, 15, 0, 3 * n), 1.0, -49152.0, True)
+                tl = tile("f", h)
+                fm = [(ps(tl, 0, n), es, ap("o1", 15, 143))] + [(ap3(tl, slice(0, 8), slice(p - 1, p + 1)), c("rr", h, 15, n * p - n, n * p), ap("pm"))
+                                                               for p in range(1, 16)]
+                mms("fa" + x, fm[:5], True, False)
+                mms("fb" + x, fm[5:9], False, False)
+                mms("fc" + x, fm[9:13], False, False)
+                mms("fd" + x, fm[13:], False, True)
+                lin("ft" + x, "S", c("ft", h), ps(tl, 0, n))
+                mms("fe" + x, [(pf, c("ft", h), ap("idf"))])
+                lin("fv" + x, "S", c("fv", h), pf, 1.0, col(10))
             else:
-                mms("y" + x, [(ps(tile, 0, n), ap("ib"), es), (ps(tile, 0, n), ap("ib"), sv)])
-                lin("yl" + x, "S", c("yl", h), ps(tile, 0, n), 4096.0, -2040.0, True)
-                for j in range(GP):
-                    part = (h, 16, 16 * gl * j, 16 * gl * (j + 1))
-                    lin("yb%d" % j + x, "S", c("yw", *part), ind(ap("mt"), c("yl", h, 1, gl * j, gl * j + gl)))
-                    op("yn%d" % j + x, "V", ("scan", c("yn", *part), ap("r16", 0, 16 * gl), c("yw", *part), 0.0, OP.mult, OP.max))
-                best = ap("yn", 2048 * h + 15, 2048 * h + 2048, 16)
-            if last:
-                lin("sn" + x, "S", c("ysf", h), best)
-                op("o.s%d" % h, "Y", ("dma", ap("ys", n * h, n * h + n), c("ysf", h)))
-                op("o.z%d" % h, "Y", ("dma", ap("yz", n * h, n * h + n), zn))
-            else:
-                sn = ap("ss", 256 * t + n * h, 256 * t + n * h + n)
-                lin("sn" + x, "V", sn, best)
-                zd = 384 * (2 * t + 2 + h)
-                op("ms" + x, "G", ("send", ap("su", 256 * t + 256 + n * h, 256 * t + 256 + n * h + n), sn, 4 * t + 2 * h))
-                op("mz" + x, "G", ("send", ap("zq", zd + 256, zd + 384), zn, 4 * t + 2 * h + 1))
-            tt("si" + x, c("si", h), ind(xw(h), ap("l2", 24 * h + 8, 24 * h + 16)), zn, OP.add)
-            ts("sj" + x, c("sj", h), c("si", h), 1, None, OP.logical_shift_right)
-            op("xc" + x, "V", ("copy", ind(ap("xt"), ap("l2", 24 * h, 24 * h + 8)), c("sj", h)))
-            if last:
+                ts("ra" + x, c("ua", h, 2, 0, n), pk, col(23), 32768.0, OP.add, OP.min)
+                lin("rb" + x, "V", c("ua", h, 2, n, 2 * n), pk, 1.0, col(14), True)
+                for nm, src, dst, m, w in (("rc", "ua", "ub", 2, 16384.0), ("rd", "ub", "uc", 4, 8192.0)):
+                    ts(nm + "0" + x, c(dst, h, 2 * m, 0, m * n), c(src, h, m), w, None, OP.min)
+                    ts(nm + "1" + x, c(dst, h, 2 * m, m * n, 2 * m * n), c(src, h, m), -w, None, OP.add)
+                ts("re0" + x, c("ud", h, 16, 0, 8 * n), c("uc", h, 8), 4096.0, -2048.0, OP.min, OP.add)
+                ts("re1" + x, c("ud", h, 16, 8 * n, 16 * n), c("uc", h, 8), 4096.0, -6144.0, OP.max, OP.add)
                 for j in range(2):
-                    lin("ch%d%d" % (h, j), "S", c("gw", h, 16, 1024 * j, 1024 * j + 1024), c("ct", h, 16, 1024 * j, 1024 * j + 1024), 1.0, -2048.0)
-                    mms("yc%d%d" % (h, j), [(ps("P:yc", 0, 256), ap("mi", 128 * m, 128 * m + 128), ap("gw", 256 * m, 256 * m + 256))
-                                            for m in range(8 * h + 4 * j, 8 * h + 4 * j + 4)], h + j == 0, h + j == 2)
-                tile = "P:yx%d" % h
-                mms("yx%d" % h, [(ps(tile, 0, n), ap("mi", 128 * m, 128 * m + 128), ap("xt", 256 * m + n * h, 256 * m + n * h + n))
-                                 for m in range(16)])
-                lin("oyx%d" % h, "S", c("oyx", h), ps(tile, 0, n))
-                op("o.x%d" % h, "Y", ("dma", ap("yx", n * h, n * h + n), c("oyx", h)))
+                    lst = []
+                    for i in range(8 * j, 8 * j + 8):
+                        p = int("{:04b}".format(i)[::-1], 2)
+                        lst.append((pf, ap("o1", 15 - p, 143 - p), c("ud", h, 16, n * i, n * i + n)))
+                    mms("f%s" % "ab"[j] + x, lst, j == 0, j == 1)
+                lin("fv" + x, "S", c("fv", h), pf, 1.0, col(14))
+            pq = ps(tile("q", h), 0, n)
+            mms("q" + x, [(pq, ap("ib"), c("hf", h)), (pq, ap("qa"), sv)])
+            ts("q1" + x, zq(h, 0), pq, -4096.0, -2048.0, OP.add, OP.max)
+        pl = ps(tile("l", 0), 0, 48)
+        mms("l", [(pl, ap("o1", 15 - b, 143 - b), ap("zq", 768 * t + b, 768 * t + 768, 16)) for b in range(16)])
+        lin("ui", "V", ap("ui", 0, 48), pl)
+        ts("uj", ap("ui", 32, 48), ap("ui", 32, 48), 15, None, OP.bitwise_and)
+        ts("uk", ap("ui", 48, 64), ap("ui", 0, 16), 3840, None, OP.bitwise_and)
+        tt("lc", ap("l2"), ap("ui"), ap("stat"), OP.add)
         if not last:
-            tt("a.%d" % t, ap("acol", 2, 3), ap("acol", 0, 1), ap("acol", 1, 2), OP.add)
-            op("da.%d" % t, "S", ("act", ap("da"), ap("i32"), AF.Identity, -15856.0, ap("acol", 2, 3), None))
-    lin("oyc", "S", ap("oyc"), ps("P:yc", 0, 256), 1.0, 2048.0 * 136)
-    op("o.c", "A", ("dma", ap("yc"), ap("oyc")))
+            op("ns", "S", ("act", ap("junk"), ap("ui", 16, 32), AF.Relu, 64.0, -32.0, ap("acol", 0, 1)))
+            lin("av", "V", ap("av"), ap("ones", 0, n), ap("acol", 0, 1), -20352.0)
+        for h in range(H):
+            x = ".%d" % h
+            sv, es = zq(h, 1), c("es", h)
+            op("cs" + x, "V", ("copy", ind(c("cf", h, 16), ap("l2", 32 + 8 * h, 40 + 8 * h)), c("fv", h)))
+            svb = sv[2][1].start
+            zn = c("zo", h) if last else ap("zs", 256 * t + n * h, 256 * t + n * h + n)
+            for j in range(4):
+                jj = "%d%d" % (j // 2, j % 2)
+                tl = tile("x" + jj, h)
+                mms("x" + jj + x, [(ap3(tl, ALL, slice(0, 1)), ap("n256"), ap("twos"))] +
+                    [(ap3(tl, ALL, slice(i, i + 1)), ap("rs", 128 * i - 128, 128 * i), ap("zq", svb + 32 * j, svb + 32 * j + 32))
+                     for i in range(1, 16)])
+                part = (h, 16, 512 * j, 512 * j + 512)
+                d = ps(tl, 0, 512)
+                if jj + x in cfg["via"]:
+                    lin("xd" + jj + x, "S", c("xd", *part), d)
+                    d = c("xd", *part)
+                op("xs" + jj + x, "V", ("scan", c("xs", *part), d, c("xw", *part), 0.0, OP.add, OP.max))
+            pz = ps(tile("zb", h), 0, n)
+            mms("xb" + x, [(pz, ap("n256"), ap("ones", 0, n)), (pz, ap("rs", 128 * 15, 128 * 16), sv)])
+            tt("zn" + x, zn, pz, c("xs", h, 16, 15, 2048, 16), OP.add)
+            py = ps(tile("y", h), 0, n)
+            sn = c("ysf", h) if last else ap("ss", 256 * t + n * h, 256 * t + n * h + n)
+            mms("y" + x, [(py, ap("ib"), es), (py, ap("i4k"), sv)])
+            lin("yl" + x, "S", c("yl", h), py, 1.0, -2040.0, True)
+            gather("ya", h, "ya", ap("mt"), c("yl", h), 0, 4)
+            for p in range(2):
+                part = (h, 16, 1024 * p, 1024 * p + 1024)
+                op("yn%d" % p + x, "V", ("scan", c("yn", *part), ap("rx"), c("ya", *part), -4096.0, OP.add, OP.max))
+            lin("sn" + x, "V", sn, c("yn", h, 16, 15, 2048, 16), 1.0, 2047.0)
+            if last:
+                op("o.s" + x, "Y", ("dma", ap("ys", n * h, n * h + n), c("ysf", h)))
+                op("o.z" + x, "Y", ("dma", ap("yz", n * h, n * h + n), zn))
+            else:
+                op("ms" + x, "G", ("send", ap("su", 256 * t + 256 + n * h, 256 * t + 256 + n * h + n), sn, 4 * t + 2 * h))
+                op("mz" + x, "G", ("send", zq(h, 2, t + 1), zn, 4 * t + 2 * h + 1))
+        if not last:
+            tt("si", ap("si"), ind(ap("xt"), ap("l2", 0, 16)), ap("zs", 256 * t, 256 * t + 256), OP.add)
+            lin("sj", "V", ap("sj"), ap("si"), 0.5, -0.25)
+            op("xc", "V", ("copy", ind(ap("xt"), ap("l2", 48, 64)), ap("sj")))
+        else:
+            mms("yx", [(ps("P:yx", 0, 256), ap("mi", 128 * m, 128 * m + 128), ap("xt", 256 * m, 256 * m + 256)) for m in range(16)])
+            lin("oyx", "S", ap("oyx"), ps("P:yx", 0, 256))
+            for h in range(H):
+                x = ".%d" % h
+                tt("si" + x, c("si", h), ind(ap("xt"), ap("l2", 8 * h, 8 * h + 8)), c("zo", h), OP.add)
+                lin("sj" + x, "V", c("sj", h), c("si", h), 0.5, -0.25)
+                pw = ps(tile("w", h), 0, n)
+                mms("wp" + x, [(pw, ap("ob"), zq(h, 0))])
+                lin("wq" + x, "V", c("hh", h), pw, 1.0 / 256, 128.5 + 1.0 / 512)
+                tt("dl" + x, c("p1", h), ind(ap("xt"), ap("l2", 48 + 8 * h, 56 + 8 * h)), c("sj", h), OP.subtract)
+                tt("dm" + x, c("p1", h), c("p1", h), c("hh", h), OP.mult)
+                tt("dn" + x, c("oyx", h), c("oyx", h), c("p1", h), OP.subtract)
+                op("o.x" + x, "Y", ("dma", ap("yx", n * h, n * h + n), c("oyx", h)))
+            for h in range(H):
+                x = ".%d" % h
+                for j in range(2):
+                    name = "ch%d" % j + x
+                    o, i = c("gw", h, 16, 1024 * j, 1024 * j + 1024), c("cf", h, 16, 1024 * j, 1024 * j + 1024)
+                    if cfg["eng"].get(name, "G") == "G":
+                        sel(name, o, i, [[0, 1024]], OP.is_ge, 0, 0)
+                    else:
+                        lin(name, "S", o, i)
+                    mms("yc%d" % j + x, [(ps("P:yc", 0, 256), ap("mi", 128 * m, 128 * m + 128), ap("gw", 256 * m, 256 * m + 256))
+                                         for m in range(8 * h + 4 * j, 8 * h + 4 * j + 4)], h + j == 0, h + j == 2)
+            lin("oyc", "S", ap("oyc"), ps("P:yc", 0, 256), 1.0, 2048.0 * 136)
+            op("o.c", "A", ("dma", ap("yc"), ap("oyc")))
     return ops
 
 
@@ -525,97 +490,52 @@ def queue_of(e):
     return "S" if e == "A" else e
 
 
-def timing(ops, K):
-    busy, after = [], []
-    for o in ops:
-        tm = sum(call_cost(cl, K) for cl in o["calls"])
-        if o["eng"] == "P":
-            tm += K["pfix"]
-        busy.append(tm)
-        after.append(K["dlat"] if o["eng"] in "YA" else K["slat"] if o["calls"][0][0] == "send" else 0.0)
-    return busy, after
+def ranks(ops, names):
+    pos = {}
+    for i, nm in enumerate(names):
+        key = nm.lstrip("+-")
+        pos[key] = i + len(names) * (nm.count("+") - nm.count("-"))
+    return [pos.get("%s@%d" % (o["key"], o["t"]), pos.get(o["key"], 0)) + len(names) * o["t"] for o in ops]
 
 
-def lag(ops, j, i, kind, K):
-    if ops[j]["eng"] == ops[i]["eng"] and ops[j]["eng"] in "VSPG" and ops[j]["calls"][0][0] != "send":
-        return K["own"] if kind and ops[j]["eng"] != "P" else 0.0
-    return K["wake"]
-
-
-def schedule(ops, preds, cfg, K, bonus=None):
+def arrange(ops, preds, rank):
     N = len(ops)
-    busy, after = timing(ops, K)
     succ = [[] for _ in range(N)]
+    left = [len(p) for p in preds]
     for i in range(N):
         for j in preds[i]:
             succ[j].append(i)
-    level = [0.0] * N
-    for i in range(N - 1, -1, -1):
-        level[i] = busy[i] + after[i] + max([level[s] + lag(ops, i, s, preds[s][i], K) for s in succ[i]] + [0.0])
-    r = cfg["seed"] * 7919 + 13
-    prio = []
-    for i in range(N):
-        r = (r * 1103515245 + 12345) % 2147483648
-        prio.append(level[i] + cfg["jit"] * (r / 2147483648.0 - 0.5) + (bonus[i] if bonus else 0.0))
-    users = {}
-    for i in range(N):
-        for b in ops[i]["tiles"]:
-            users.setdefault(b, []).append(i)
-    left = [len(p) for p in preds]
     ready = [i for i in range(N) if left[i] == 0]
-    end = [0.0] * N
-    done = [False] * N
-    free = {}
-    holder = [None] * 8
-    bank = {}
     order = []
-    rt = {i: 0.0 for i in ready}
     while ready:
-        cand = []
-        for i in ready:
-            e = ops[i]["eng"]
-            st = max(rt[i], free.get("Y" if e == "A" else e, 0.0), free.get("S", 0.0) if e == "A" else 0.0)
-            bk = None
-            new = [b for b in ops[i]["tiles"] if b not in bank]
-            if new:
-                pool = range(cfg["xbanks"]) if new[0][2] == "x" else range(cfg["xbanks"], 8)
-                opts = []
-                for b in pool:
-                    hd = holder[b]
-                    if hd is None:
-                        opts.append((0.0, b))
-                    elif all(done[u] for u in users[hd]):
-                        opts.append((max(end[u] for u in users[hd]) + K["wake"], b))
-                if not opts:
-                    continue
-                tb, bk = min(opts)
-                st = max(st, tb)
-            cand.append((st, i, bk))
-        if not cand:
-            return None
-        t0, i0, _b = min(cand)
-        q = queue_of(ops[i0]["eng"])
-        st, i, bk = max([cd for cd in cand if queue_of(ops[cd[1]]["eng"]) == q and cd[0] <= t0 + cfg["delta"]], key=lambda cd: prio[cd[1]])
-        if bk is not None:
-            b = [b for b in ops[i]["tiles"] if b not in bank][0]
-            bank[b] = bk
-            holder[bk] = b
-        e = ops[i]["eng"]
-        if e == "A":
-            free["S"] = st + 60.0
-            free["Y"] = st + busy[i]
-        else:
-            free[e] = st + busy[i]
-        end[i] = st + busy[i] + after[i]
-        done[i] = True
-        order.append(i)
+        i = min(ready, key=lambda v: (rank[v], v))
         ready.remove(i)
+        order.append(i)
         for s in succ[i]:
             left[s] -= 1
             if left[s] == 0:
                 ready.append(s)
-                rt[s] = max(end[j] + lag(ops, j, s, kd, K) for j, kd in preds[s].items())
-    return order, bank, max(end)
+    return order
+
+
+def pool(tile):
+    return range(FLAT) if tile[2] == "x" else range(FLAT, 8) if tile[2] == "f" else range(8)
+
+
+def banks(ops, order):
+    lastuse = {}
+    for p, i in enumerate(order):
+        for b in ops[i]["tiles"]:
+            lastuse[b] = p
+    until, bank = [-1] * 8, {}
+    for p, i in enumerate(order):
+        for b in ops[i]["tiles"]:
+            if b not in bank:
+                k = min(pool(b), key=lambda v: until[v])
+                assert until[k] < p
+                bank[b] = k
+                until[k] = lastuse[b]
+    return bank
 
 
 def with_banks(ops, preds, order, bank):
@@ -636,6 +556,7 @@ def with_banks(ops, preds, order, bank):
 
 def waits(ops, full, order):
     pos, cnt = {}, {}
+    where = {i: p for p, i in enumerate(order)}
     for i in order:
         o = ops[i]
         own = o["eng"] in "YA" or o["calls"][0][0] == "send"
@@ -656,7 +577,7 @@ def waits(ops, full, order):
             if kn.get(key, 0) < p and want.get(key, (0, 0))[0] < p:
                 want[key] = (p, j)
         lst = []
-        for key, (p, j) in sorted(want.items(), key=lambda kv: -order.index(kv[1][1])):
+        for key, (p, j) in sorted(want.items(), key=lambda kv: -where[kv[1][1]]):
             if kn.get(key, 0) >= p:
                 continue
             lst.append(j)
@@ -680,30 +601,10 @@ def plan():
     if not PLAN:
         ops = build(CFG)
         preds = edges(ops)
-        if CFG["order"]:
-            o = CFG["order"]
-            order = [int(o[i:i + 2], 36) for i in range(0, len(o), 2)]
-            bank = banks(ops, order)
-        else:
-            order, bank, _t = schedule(ops, preds, CFG, COST)
+        order = arrange(ops, preds, ranks(ops, ROUND.split()))
+        bank = banks(ops, order)
         PLAN["p"] = (ops, order, bank, waits(ops, with_banks(ops, preds, order, bank), order))
     return PLAN["p"]
-
-
-def banks(ops, order):
-    lastuse = {}
-    for p, i in enumerate(order):
-        for b in ops[i]["tiles"]:
-            lastuse[b] = p
-    until, bank = [-1] * 8, {}
-    for p, i in enumerate(order):
-        for b in ops[i]["tiles"]:
-            if b not in bank:
-                k = until.index(min(until))
-                assert until[k] < p
-                bank[b] = k
-                until[k] = lastuse[b]
-    return bank
 
 
 def lanes_engines(topo, src, dst):
@@ -728,7 +629,14 @@ def rank_program(g, core, T, topo):
             return a
         if a[0] == "ind":
             return R(a[1]).indirect(R(a[2]))
-        return T["ps%d" % bank[a[1]] if a[1].startswith("P:") else a[1]][a[2]]
+        if not a[1].startswith("P:"):
+            return T[a[1]][a[2]]
+        if bank[a[1]] >= FLAT:
+            return T["ps%d" % bank[a[1]]][a[2]]
+        cs = cols(a)
+        step = int(cs[1] - cs[0])
+        assert (np.diff(cs) == step).all()
+        return T["ps%d" % bank[a[1]]][:, int(cs[0]):int(cs[-1]) + 1:step]
 
     waited = set(j for i in order for j in need[i])
     sig, cnt, nd, sent = {}, {}, [0], [0]

import numpy as np
from concourse.mybir import AluOpType as OP, ActivationFunctionType as AF

LEVELS, H, n = 4, 2, 128
F32, BF, F16, I32, U16 = "float32", "bfloat16", "float16", "int32", "uint16"
SB = {
    "cr": (4096, I32), "ct": (4096, I32), "cf": (4096, F32), "mt": (4104, I32), "xt": (4096, BF),
    "s0i": (256, I32), "z0b": (256, BF),
    "gw": (4096, F16), "xw": (4096, BF), "es": (256, F16), "eq": (2048, F16), "p1": (256, F32), "p2": (256, I32),
    "hh": (256, I32), "h16": (256, U16), "hf": (256, F16), "s4": (256, F16), "tf": (768, F16), "sg": (256, BF),
    "sr": (256, BF), "tr": (256, BF), "rr": (2 * 1920, F32), "ft": (256, F32), "fv": (256, F32),
    "ua": (512, U16), "ub": (1024, U16), "uc": (2048, U16), "ud": (4096, F16),
    "ui": (64, I32), "l2": (64, U16), "xs": (4096, F16), "xd": (4096, BF), "yl": (256, U16), "ya": (4096, F16),
    "yn": (4096, F16), "si": (256, I32), "sj": (256, I32), "zq": (4 * 768, F16), "su": (1024, U16), "zs": (768, F16),
    "zo": (256, BF), "ss": (768, U16), "ysf": (256, F32), "junk": (16, BF), "acol": (8, F32), "av": (128, F16),
    "oyx": (256, F32), "oyc": (256, F32),
    "ones": (256, BF), "twos": (32, BF), "idf": (128, F32), "ib": (128, BF), "i4k": (128, BF), "n4k": (128, BF),
    "i33": (128, BF), "n256": (128, BF), "ob": (128, BF), "o2k": (128, BF), "lo": (128, BF), "up": (128, BF),
    "u4k": (128, BF), "tm": (128, BF), "qa": (128, BF), "s3m": (128, BF), "wd": (2304, BF), "w0": (1152, BF),
    "o1": (144, BF), "bw": (144, BF), "dm": (1024, BF), "ad": (1024, F16), "rs": (2048, BF), "r0": (1024, BF),
    "mi": (2048, BF), "rx": (1024, BF), "stat": (64, F32), "a16": (32, F32),
    "raw": (80, F32), "cy": (64, F32), "sm": (80, F32), "pm": (16, F32), "tie": (48, F32), "m4": (16, F32),
    "im": (128, BF), "qi": (8, I32), "qf": (24, F32), "dd": (8, F32), "tau": (24, F32),
}
SCRATCH = {k: ("sbuf", [128, v[0]], v[1]) for k, v in SB.items()}
SCRATCH["zz"] = ("sbuf", [128, 8, 32], BF)
SCRATCH["st"] = ("sbuf", [128, 5, 8, 16], BF)
FLAT = 6
for _b in range(8):
    SCRATCH["ps%d" % _b] = ("psum", [128, 512] if _b < FLAT else [128, 32, 16], F32)
SEMAPHORES = (["V", "S", "P", "G", "left"] + ["ar%d" % i for i in range(12)] + ["d%d" % i for i in range(24)])
DRAM = {"x0": (4096, BF), "cm": (4096, I32), "s0": (256, I32), "z0": (256, BF),
        "yx": (256, F32), "yc": (256, F32), "ys": (256, F32), "yz": (256, BF)}
ALL = slice(None)
COLS = {}

CFG = {
    "blocks": (0, 1280, 2560, 3584, 4096),
    "parts": {"gc": (4, 4), "gx": (4, 4), "ya": (4, 4)},
    "sort": "FF",
    "via": (),
    "ne": 8,
}
ROUND = 'p2.1 r0.1@0 -k.lo r1.1@0 -k.q2 k.st1 -k.wd0 -k.qf -k.dm5 -k.dm7 -k.wd2 tf2.0 s1.0 oyx sg.0 s2.0 hh.1 h16.1 gx0.1 k.n4k hf.1 sr.0 tf0.0@0 tf2.0@0 tf1.0@0 s3.0 s1.0@0 sv.0 p2.1@0 k.n256 hh.1@0 h16.1@0 gx0.1@0 sg.0@0 s2.0@0 k.rt1 hf.1@0 sr.0@0 -k.twos -k.t1 -k.fb0 gx1.1@0 gx1.1 gx2.1 y.0 x10.0 q.0@3 s3.0@0 y.0@3 -k.fb1 -k.b1 -k.t2 -k.b0 -k.t3 -k.b2 gx3.1 sv.0@0 -k.t4 yl.0 yl.0@3 ya1.0@3 bn0.1 q.0@0 t.0@3 y.0@0 gx2.1@0 tr.0@3 ya2.0@3 t.0 ya0.0 gx3.1@0 bn0.1@0 t.0@0 x10.0@0 ya3.0 ya1.0 yl.0@0 bn1.1 xs10.0 tr.0 s4.1 q.0 +o.x.0 k.0 bn1.1@0 x01.0 ya0.0@3 k.st20 tr.0@0 tf2.1 tf0.1 x01.0@3 x11.0@0 x10.0@3 -m0 -k.dq -k.ad5 -k.fb2 -k.ad4 -k.ad7 -k.ad8 tf1.1 q1.0@3 ra.0 rb.0 ya2.0 q1.0@0 ya0.0@0 ya2.0@0 ya1.0@0 -k.k32 -k.pm0 -k.s3 -k.rb -k.pm1 -k.b3 s4.1@0 k.st21 x01.0@0 tf1.1@0 tf2.1@0 tf0.1@0 s1.1@0 xs01.0@3 xs10.0@0 xs01.0@0 xs01.0 s1.1 k.0@0 ya3.0@0 yn1.0 k.0@3 sg.1 sg.1@0 s2.1@0 sr.1@0 x11.0 x00.0@0 -c0 -k.ad6 -k.ad3 -k.i33 yn1.0@0 +o.x.1 wp.0 -m1 s3.1@0 rc.0 --ld.c0 --ld.z s2.1 x00.0@3 ra.0@3 rb.0@3 --ld.s ra.0@0 sv.1@0 sr.1 x00.0 s3.1 rb.0@0 rc.0@0 rd.0@0 rf.0@0 re.0@0 yn0.0@0 fa.0@0 y.1@0 yl.1@0 re.0 rd.0 fa.0 q.1@0 t.1@0 xs10.0@3 +oyc xb.0@0 x11.1@0 yn0.0@3 sv.1 rc.0@3 y.1 q1.1@0 tr.1@0 t.1 fb.0 q.1 ya0.1@0 ya2.1@0 sn.0@0 ya1.1@0 k.1@0 xb.1@0 l@0 fb.0@0 ui@0 xs11.0@0 yn0.1@0 ra.1@0 -k.s3m -k.s4 -av0 rb.1@0 ya3.1@0 yn1.1@0 uk@0 rf.0 tr.1 k.1 x11.1 fc.0 fd.0 yn0.0 q1.0 yl.1 sn.0 -k.ad2 -k.ad1 ya2.1 ya0.1 wq.0 ya1.1 re.0@3 rf.0@3 ya3.1 q1.1 +o.c yn0.1 l xb.0 sn.1@0 ra.1 rc.1@0 rd.1@0 ya3.0@3 rb.1 xb.0@3 x11.0@3 q.1@3 t.1@3 y.1@3 rd.0@3 tr.1@3 q1.1@3 x11.1@3 yl.1@3 fa.0@3 xs11.0@3 re.1@0 rf.1@0 yn1.0@3 xs11.1@3 rc.1 rd.1 re.1 -su0 -k.dq2 fc.0@0 fd.0@0 rf.1 ft.0 ya3.1@3 l@3 k.1@3 fa.1@0 fb.1@0 fc.1@0 fd.1@0 ra.1@3 ya0.1@3 rb.1@3 ui fa.1 fb.1 fb.0@3 x01.1@3 xs00.0@3 ya1.1@3 ns fc.0@3 fd.0@3 --ld.c1 zn.0@3 ui@3 -k.tie x00.1@3 ft.0@3 yn1.1 fc.1 xs00.0 fd.1 ft.0@0 fe.0 ft.1@0 ms.0 xb.1 ms.0@0 sn.1 uj@3 uk@3 fe.0@0 yn0.1@3 fe.1@0 fv.0@0 rc.1@3 ya2.1@3 rd.1@3 xs00.0@0 xs11.1 xs11.0 ft.1 fv.0 -cf0 -k.ti2 x10.1@0 ms.1@0 uk fe.1 av re.1@3 rf.1@3 sn.0@3 fe.0@3 wp.1 xb.1@3 fa.1@3 uj@0 xs01.1@3 fv.1@0 yn1.1@3 -c1 ns@0 fb.1@3 uj x01.1@0 fv.0@3 -k.s5 -k.qa -z0 -k.s7 -k.s61 -k.s60 zn.0@0 fc.1@3 fd.1@3 x00.1@0 lc@3 xs00.1@3 si.0 lc@0 -k.s8 -k.i4k -c2 -k.s62 -k.st0 mz.0@0 zn.0 ms.1 fv.1 lc -k.dm4 cs.0@3 x01.1 cs.0 -k.dm6 -k.wd1 av@0 -k.dm3 cs.1 xs01.1 wq.1 xs11.1@0 cs.0@0 x00.1 cs.1@0 -gc1.0 xs10.1@0 -gc0.0 x10.1 xs00.1 xs01.1@0 xs00.1@0 -gc2.0 xs10.1 -d10.0 mz.0 k.mi00 k.mi10 -c3 sn.1@3 --ld.c2 -cf3 -k.sx0 -k.bw -cf1 -k.ti1 -k.dm1 -k.up -cf2 -k.dm2 -k.dm8 -k.ti3 -k.ra ch1.0 --k.m4 --k.q ft.1@3 -gc3.0 -gc0.0@0 -d11.0 fe.1@3 fv.1@3 -k.rs2 zn.1@0 -gc1.0@0 -gc3.0@0 si@0 cs.1@3 x10.1@3 xs10.1@3 --ld.c3 sj.0 zn.1@3 -d10.0@0 si.1 dl.0 o.s.0 -gc2.1@0 sj.1 mz.1@0 -u.0 ch0.0 -gc2.0@0 -d11.0@0 ch0.1 -gc1.1 -gc0.1 -es.0@0 o.z.0 -gc2.1 -gc3.1 zn.1 si dm.0 dl.1 -es.0 mz.1 --k.ones --k.rs0 --k.q1 k.mi01 k.mi11 k.mi02 k.mi12 k.mi03 -gc0.1@0 -u.1@0 -m3 -gc1.1@0 -u.0@0 -k.ti4 -gc3.1@0 sj@0 -p1.0@0 -k.sx1 -k.ti5 -df0.0@0 k.mi13 --ld.x -eq0.0@0 yc0.0 -df0.0 -df1.0 -k.ti6 -df1.0@0 -eq1.0@0 -k.rx0 o.s.1 o.z.1 -k.rs1 yc1.0 ch1.1 -r0.0@0 sj -p1.0 -eq0.0 -eq1.0 -d10.1 -r0.0 -r1.0 yc0.1 yc1.1 -d11.1 xc -yx xc@0 -r1.0@0 -p2.0@0 -es.1 -df0.1 -d10.1@0 -k.ti7 -d11.1@0 -df1.1 -p2.0 --k.ob1 --k.s0 --k.im --k.dd -k.rt2 -hh.0 --k.ob2 -h16.0 -gx0.0 -m2 -gx1.0 --k.q3 --k.s1 -gx2.0 -hh.0@0 --k.q4 -k.tm0 -h16.0@0 -k.sx2 --k.a16 -gx3.0 -u.1 -eq0.1 -k.sx3 -gx1.0@0 -k.tm1 -es.1@0 -k.rx1 -gx3.0@0 -df1.1@0 -df0.1@0 -eq1.1 -bn0.0 -k.qa1 -gx0.0@0 --k.s2 --k.w --k.o2k --k.o10 -bn1.0 --k.ib -bn0.0@0 -m4 -r0.1 -p1.1@0 -gx2.0@0 -k.sx4 -eq0.1@0 -k.sx5 -bn1.0@0 -s4.0@0 --k.zz -eq1.1@0 -r1.1 -k.sx6 -hf.0@0 -k.idf -k.sx7 -hf.0 -k.ti8 -k.u4k -p1.1 dn.0 --k.o1 dm.1 dn.1 -s4.0 -tf1.0 -tf0.0'
ENG = 'av:S cf3:V ch0.0:G ch0.1:S ch1.1:S es.0:V es.1@0:V ft.0@3:V fv.1@3:V gc1.0@0:V gc2.0:V gc2.0@0:S gc2.1@0:V gc3.0@0:V gx0.0:V gx0.1:V gx2.0:V gx2.1@0:V gx3.1:V gx3.1@0:S k.i4k:V k.n256:V k.s3m:V k.sx0:V k.sx1:V k.sx2:V k.sx4:V m1:S m2:S m3:S m4:S ra.0:V ra.0@0:S ra.0@3:S rb.0:V rb.0@0:S rb.0@3:S s4.1:V sg.0:S sg.1:S sj.0:S sn.0@3:S sn.1@3:S sr.1@0:V tf2.0:S tf2.0@0:V tr.0:V tr.0@3:S tr.1@0:V tr.1@3:V ui:S ui@0:V ui@3:V wq.0:S wq.1:S ya0.1:V ya0.1@3:S ya1.0@0:V ya1.0@3:V ya1.1:V ya1.1@0:S ya2.0:V ya2.0@0:S ya2.0@3:S ya2.1@0:V ya3.0@3:V yl.0:V yl.1:V yl.1@3:S'
CFG["eng"] = dict(v.split(":") for v in ENG.split())


def ap(name, a=None, b=None, s=None):
    return ("ap", name, (ALL, slice(a, b, s)))


def ap3(name, i, j, part=ALL):
    return ("ap", name, (part, i, j))


def ps(tile, a, b):
    return ("ap", tile, (ALL, slice(a // 16, b // 16), ALL))


def ind(win, off):
    return ("ind", win, off)


def shape_of(name):
    if name.startswith("P:"):
        return [128, 32, 16], F32
    if name in DRAM:
        return [128, DRAM[name][0]], DRAM[name][1]
    return SCRATCH[name][1], SCRATCH[name][2]


def cols(a):
    key = ("P:" if a[1].startswith("P:") else a[1], str(a[2]))
    if key not in COLS:
        sh = shape_of(a[1])[0]
        COLS[key] = np.arange(int(np.prod(sh[1:]))).reshape(sh[1:])[a[2][1:]].reshape(-1)
    return COLS[key]


def isap(a):
    return isinstance(a, tuple) and len(a) == 3 and a[0] in ("ap", "ind")


def build(cfg):
    ops = []
    cfg["free"] = {}
    lev = [0]

    def op(name, eng, *calls):
        ops.append({"key": name, "t": lev[0], "eng": eng, "calls": list(calls)})

    def eng(name, dflt):
        cfg["free"][name] = dflt
        return cfg["eng"].get("%s@%d" % (name, lev[0]), cfg["eng"].get(name, dflt))

    def lin(name, dflt, out, in_, scale=1.0, bias=0.0, relu=False):
        if eng(name, dflt) == "S":
            op(name, "S", ("act", out, in_, AF.Relu if relu else AF.Identity, bias, scale, None))
        elif relu and shape_of(out[1])[1] != U16:
            assert scale == 1.0
            op(name, "V", ("ts", out, in_, bias, 0.0, OP.add, OP.max))
        elif not isap(scale) and scale == 1.0 and not isap(bias) and bias == 0.0:
            op(name, "V", ("copy", out, in_))
        elif not isap(scale) and scale == 1.0:
            op(name, "V", ("ts", out, in_, bias, None, OP.add, None))
        else:
            op(name, "V", ("ts", out, in_, scale, bias, OP.mult, OP.add))

    def ts(name, out, in_, s1, s2, o0, o1=None):
        op(name, "V", ("ts", out, in_, s1, s2, o0, o1))

    def tt(name, out, a, b, o):
        op(name, "V", ("tt", out, a, b, o))

    def fill(name, out, v):
        op(name, "V", ("memset", out, v))

    def mms(name, lst, first=True, last=True):
        op(name, "P", *[("mm", o, l, r, first and i == 0, last and i == len(lst) - 1) for i, (o, l, r) in enumerate(lst)])

    def col(j):
        return ap("qf", j, j + 1)

    def sel(name, out, in_, pat, cmp, base, ch, v=0.0):
        op(name, "G", ("sel", out, in_, pat, cmp, v, base, ch))

    def diag(name, out, in_, v):
        op(name, "G", ("sel", out, in_, [[-1, 128]], OP.not_equal, v, 0, 1))

    def iota(name, out, pat, base, ch):
        op(name, "G", ("iota", out, pat, base, ch))

    def gather(name, h, out, win, lst, p0, p1):
        m = cfg["parts"][name][h]
        w = n // m
        for p in range(p0 * m // 4, p1 * m // 4):
            a = lst[2][1].start + w * p
            lin("%s%d.%d" % (name, p, h), "S", c(out, h, 16, 16 * w * p, 16 * w * p + 16 * w), ind(win, ap(lst[1], a, a + w)))

    def st(j):
        return ("ap", "st", (ALL, j, ALL, ALL))

    def c(name, h, m=1, a=0, b=None, s=None):
        return ap(name, m * n * h + a, m * n * h + (m * n if b is None else b), s)

    bl = cfg["blocks"]
    op("ld.s", "A", ("dma", ap("s0i"), ap("s0")))
    op("ld.z", "A", ("dma", ap("z0b"), ap("z0")))
    for j in range(len(bl) - 1):
        op("ld.c%d" % j, "Y", ("dma", ap("cr", bl[j], bl[j + 1]), ap("cm", bl[j], bl[j + 1])))
    op("ld.x", "Y", ("dma", ap("xt"), ap("x0")))
    for j in range(len(bl) - 1):
        ts("c%d" % j, ap("ct", bl[j], bl[j + 1]), ap("cr", bl[j], bl[j + 1]), 4095, None, OP.bitwise_and)
        lin("cf%d" % j, "S", ap("cf", bl[j], bl[j + 1]), ap("ct", bl[j], bl[j + 1]), 1.0, -2048.0)
    lin("su0", "S", ap("su", 0, 256), ap("s0i"))
    lin("z0", "S", ap("zq", 512, 768), ap("z0b"))
    fill("av0", ap("av"), -20352.0)
    fill("m0", ap("mt", 0, 8), -2047)
    for j in range(len(bl) - 1):
        lin("m%d" % (j + 1), "V", ap("mt", 8 + bl[j], 8 + bl[j + 1]), ap("cr", bl[j], bl[j + 1]), 1.0 / 4096, -2047.5 + 1.0 / 8192)

    fill("k.ones", ap("ones"), 1.0)
    fill("k.twos", ap("twos"), 2.0)
    fill("k.wd0", ap("w0"), 1.0)
    for j in range(2):
        sel("k.wd%d" % (j + 1), ap("wd", 1152 * j, 1152 * j + 1152), ap("w0"),
            [[-1, 8], [-16, 9], [1000, 16]], OP.is_equal, -15000 - 8 * j, 1)
    sel("k.ib", ap("ib"), ap("ones", 0, 128), [[-1, 128]], OP.is_equal, 0, 1)
    sel("k.zz", ap3("zz", ALL, ALL), ap("ones"), [[-16, 8], [0, 2], [-1, 16]], OP.is_equal, 0, 1)
    sel("k.ob1", ap("ob"), ap("ones", 0, 128), [[-16, 8], [0, 16]], OP.is_ge, 0, 1)
    sel("k.ob2", ap("ob"), ap("ob"), [[16, 8], [0, 16]], OP.is_ge, 15, -1)
    sel("k.lo", ap("lo"), ap("ob"), [[1, 128]], OP.is_gt, 0, -1)
    sel("k.up", ap("up"), ap("ob"), [[-1, 128]], OP.is_gt, 0, 1)
    iota("k.q", ap("qi", 0, 1), [[0, 1]], 0, 1)
    iota("k.dd", ap("dd"), [[1, 8]], 1, 0)
    iota("k.im", ap("im"), [[1, 128]], 0, 0)
    ts("k.q1", ap("qi", 1, 2), ap("qi", 0, 1), 15, None, OP.bitwise_and)
    ts("k.q2", ap("qi", 2, 3), ap("qi", 0, 1), 2, 3, OP.logical_shift_right, OP.bitwise_and)
    ts("k.q3", ap("qi", 3, 4), ap("qi", 0, 1), 3, None, OP.bitwise_and)
    lin("k.qf", "V", ap("qf", 0, 4), ap("qi", 0, 4))
    for d in range(1, 9):
        diag("k.dm%d" % d, ap("dm", 128 * d - 128, 128 * d), ap3("zz", ALL, slice(d, d + 16)), -1.0)
    ts("k.t1", ap("tau", 0, 8), ap("dd"), col(1), 15.0, OP.add, OP.is_le)
    tt("k.t2", ap("tau", 8, 16), ap("tau", 0, 8), ap("dd"), OP.mult)
    ts("k.t3", ap("tau", 16, 24), ap("tau", 8, 16), col(0), None, OP.add)
    ts("k.t4", col(4), ap("tau", 7, 8), 19616.0, None, OP.mult)
    for d in range(1, 9):
        ts("k.ad%d" % d, ap("ad", 128 * d - 128, 128 * d), ap("im"), ap("tau", 15 + d, 16 + d),
           col(4) if d == 8 else 19616.0, OP.is_equal, OP.mult)
    for name, src, v in (("o2k", "ob", 2048.0), ("i33", "ib", 33.0), ("i4k", "ib", 4096.0), ("n4k", "ib", -4096.0),
                         ("n256", "ib", -256.0), ("u4k", "up", 4096.0), ("idf", "ib", 1.0), ("qa", "lo", -4096.0)):
        lin("k." + name, "S", ap(name), ap(src), v)
    diag("k.qa1", ap("qa"), ap("qa"), 4096.0)
    tt("k.tm0", ap("tm"), ap("up"), ap("lo"), OP.subtract)
    diag("k.tm1", ap("tm"), ap("tm"), 32.0)
    fill("k.o10", ap("o1"), 0.0)
    lin("k.o1", "S", ap("o1", 15, 143, 16), ap("ob", 0, 128, 16))
    ts("k.q4", ap("qi", 4, 5), ap("qi", 0, 1), 1, None, OP.bitwise_and)
    lin("k.w", "S", col(5), ap("qi", 4, 5), -0.5, 0.25)
    lin("k.bw", "S", ap("bw"), ap("o1"), col(5))
    sel("k.s0", ap("raw", 16, 80), ap("ones", 0, 64), [[-1, 4], [0, 4], [1, 4]], OP.is_equal, 0, 0)
    sel("k.s1", ap("raw", 16, 80), ap("raw", 16, 80), [[-1, 4], [1, 4], [0, 4]], OP.not_equal, 0, 0, -1.0)
    sel("k.s2", ap("raw", 16, 80), ap("raw", 16, 80), [[-6, 4], [1, 4], [5, 4]], OP.not_equal, 0, 0, 1.0)
    lin("k.s3", "S", ap("raw", 0, 16), ap("raw", 64, 80))
    tt("k.s4", ap("cy"), ap("raw", 16, 80), ap("raw", 0, 64), OP.subtract)
    lin("k.s5", "S", ap("sm", 0, 16), ap("cy", 16, 32), 4.0)
    for j, c0 in enumerate((0, 48, 32)):
        tt("k.s6%d" % j, ap("sm", 16 + 16 * j, 32 + 16 * j), ap("cy", c0, c0 + 16), ap("cy", 16, 32), OP.subtract)
    iota("k.tie", ap("tie", 0, 16), [[-2, 4], [2, 4]], -1, 0)
    lin("k.ti1", "S", ap("tie", 0, 16), ap("tie", 0, 16), 1.0 / 8)
    lin("k.ti2", "S", ap("tie", 16, 32), ap("raw", 16, 32), 16.0)
    lin("k.ti3", "S", ap("tie", 32, 48), ap("cy", 16, 32), 98304.0)
    tt("k.ti4", ap("tie", 0, 16), ap("tie", 0, 16), ap("tie", 16, 32), OP.add)
    tt("k.ti5", ap("tie", 0, 16), ap("tie", 0, 16), ap("tie", 32, 48), OP.add)
    ts("k.ti6", ap("tie", 16, 32), ap("im", 0, 16), col(1), None, OP.is_equal)
    tt("k.ti7", ap("tie", 0, 16), ap("tie", 0, 16), ap("tie", 16, 32), OP.mult)
    op("k.ti8", "S", ("act", ap("tie", 32, 48), ap("tie", 0, 16), AF.Identity, 0.0, 1.0, col(12)))
    iota("k.m4", ap("m4"), [[1, 4], [0, 4]], 0, 0)
    tt("k.dq", col(6), col(2), col(3), OP.is_equal)
    lin("k.dq2", "S", col(11), col(6), 4.0, 1.0)
    ts("k.s7", ap("sm", 64, 80), ap("m4"), col(2), col(11), OP.is_equal, OP.mult)
    ts("k.s8", ap("sm", 64, 80), ap("sm", 64, 80), col(6), None, OP.subtract)
    lin("k.pm0", "S", ap("pm", 0, 16, 2), ap("ob", 0, 128, 16), -1.0)
    lin("k.pm1", "S", ap("pm", 1, 16, 2), ap("ob", 0, 128, 16))
    for j in range(8):
        lin("k.sx%d" % j, "S", ("ap", "st", (ALL, ALL, j, ALL)), ap("sm"), ap("pm", 2 * j + 1, 2 * j + 2))
    ts("k.b0", col(17), col(3), 0.0, col(2), OP.is_equal, OP.mult)
    ts("k.b1", col(18), col(3), 1.0, -6144.0, OP.is_equal, OP.mult)
    tt("k.b2", col(19), col(17), col(18), OP.add)
    lin("k.b3", "S", col(20), col(19), 0.25)
    lin("k.s3m", "S", ap("s3m"), ap("ob"), col(20))
    lin("k.k32", "S", col(7), col(1), 1.0, -32.0)
    if "F" in cfg["sort"]:
        ts("k.fb0", col(8), col(1), 0.0, 524288.0, OP.is_equal, OP.mult)
        lin("k.fb1", "S", col(9), col(1), 4096.0, -63488.0)
        tt("k.fb2", col(10), col(8), col(9), OP.add)
        lin("k.ra", "S", col(21), col(1), 4096.0, -2048.0)
        lin("k.rb", "S", col(22), col(1), 4096.0, -6144.0)
    if "U" in cfg["sort"]:
        lin("k.ua", "S", col(23), col(1), 4096.0, 2048.0)
        lin("k.ub", "S", col(14), col(1), 4096.0, -30720.0)
    iota("k.a16", ap("a16"), [[16, 32]], 0, 0)
    fill("k.st0", ap("stat", 0, 32), 32768.0)
    ts("k.st1", ap("stat", 48, 64), ap("a16", 0, 16), col(1), None, OP.add)
    for h in range(H):
        ts("k.st2%d" % h, ap("stat", 32 + 8 * h, 40 + 8 * h), ap("stat", 48, 56), 16.0, None, OP.mult)
    fill("k.rs0", ap("r0"), 256.0)
    for j in range(2):
        sel("k.rs%d" % (j + 1), ap("rs", 1024 * j, 1024 * j + 1024), ap("r0"), [[-1, 8], [-16, 8], [0, 16]], OP.is_equal, -8 * j, 1)
        sel("k.rt%d" % (j + 1), ap("rs", 1024 * j, 896 * j + 1024), ap("rs", 1024 * j, 896 * j + 1024),
            [[-1, 8 - j], [-16, 8], [0, 16]], OP.not_equal, -8 * j - 1, 1, -256.0)
    fill("k.rx0", ap("rx"), 0.0)
    fill("k.rx1", ap("rx", 0, 1024, 16), -4096.0)
    for j in range(4):
        iota("k.mi0%d" % j, ap("mi", 512 * j, 512 * j + 512), [[1, 4], [0, 128]], 1 + 4 * j, 0)
        sel("k.mi1%d" % j, ap("mi", 512 * j, 512 * j + 512), ap("mi", 512 * j, 512 * j + 512), [[0, 4], [-1, 128]], OP.is_equal, 0, 1)

    for t in range(LEVELS):
        lev[0] = t
        last = t == LEVELS - 1

        def zq(h, j, tt_=t):
            a = 768 * tt_ + n * (2 * j + h)
            return ap("zq", a, a + n)

        def tile(name, h):
            return "P:%s%d.%d" % (name, t, h)

        for h in range(H):
            x = ".%d" % h
            z = zq(h, 2)
            for j in range(2):
                gather("gc", h, "gw", ap("cf"), ap("su", 256 * t + n * h, 256 * t + n * h + n), 2 * j, 2 * j + 2)
                mms("d1%d" % j + x, [(ps(tile("e", h), 64 * j, 64 * j + 64),
                                      ap("wd", 144 * ((k + t) & 15) + 15 - k, 144 * ((k + t) & 15) + 143 - k),
                                      c("gw", h, 16, 1024 * j + k, 1024 * j + 1024, 16)) for k in range(16)], j == 0, j == 1)
            es = c("es", h)
            lin("es" + x, "S", es, ps(tile("e", h), 0, n))
            pu = ps(tile("u", h), 0, n)
            mms("u" + x, [(pu, ap("ob"), z)])
            tt("p1" + x, c("p1", h), pu, es, OP.mult)
            for j in range(2):
                tl = tile("d%d" % j, h)
                mms("df%d" % j + x, [(ps(tl, n * i, n * i + n), ap("dm", 512 * j + 128 * i, 512 * j + 128 * i + 128), es) for i in range(4)])
                ts("eq%d" % j + x, c("eq", h, 8, 512 * j, 512 * j + 512), ps(tl, 0, 512), 0.0, None, OP.is_equal)
            pr = ps(tile("r", h), 0, n)
            pairs = [(pr, ap("ad", 128 * d, 128 * d + 128), c("eq", h, 8, n * d, n * d + n)) for d in range(8)]
            mms("r0" + x, [(pr, ap("ob"), ap("av")), (pr, ap("o2k"), z), (pr, ap("i33"), es)] + pairs[:4], True, False)
            mms("r1" + x, pairs[4:], False, True)
            tt("p2" + x, c("p2", h), pr, c("p1", h), OP.add)
            ts("hh" + x, c("hh", h), c("p2", h), 5, 4095, OP.arith_shift_right, OP.bitwise_and)
            lin("h16" + x, "V", c("h16", h), c("hh", h))
            lin("hf" + x, "S", c("hf", h), c("hh", h), 1.0, -2048.0)
            pb = ps(tile("b", h), 0, n)
            for j in range(2):
                gather("gx", h, "xw", ap("xt"), c("h16", h), 2 * j, 2 * j + 2)
                mms("bn%d" % j + x, [(ps(tile("b", h), 64 * j, 64 * j + 64), ap("bw", 15 - k, 143 - k),
                                      c("xw", h, 16, 1024 * j + k, 1024 * j + 1024, 16)) for k in range(16)], j == 0, j == 1)
            s4 = c("s4", h)
            lin("s4" + x, "S", s4, pb)
            for j in range(3):
                lin("tf%d" % j + x, "V", c("tf", h, 3, n * j, n * j + n), s4, 1.0, 1535.625 + 0.25 * j)
            p1 = ps(tile("s1", h), 0, n)
            mms("s1" + x, [(p1, st(0), s4)] + [(p1, st(j + 1), c("tf", h, 3, n * j, n * j + n)) for j in range(3)])
            signs = eng("sg" + x, "V") == "S"
            if signs:
                op("sg" + x, "S", ("act", c("sg", h), p1, AF.Sign, col(12), 1.0, None))
            else:
                ts("sg" + x, c("sg", h), p1, col(12), 0.0, OP.add, OP.is_gt)
            p2 = ps(tile("s2", h), 0, n)
            mms("s2" + x, [(p2, st(4), c("sg", h))])
            if eng("sr" + x, "S") == "S":
                op("sr" + x, "S", ("act", c("sr", h), p2, AF.Relu, -1.0 if signs else -3.0, 0.5 if signs else 1.0, None))
            else:
                ts("sr" + x, c("sr", h), p2, 4.0, None, OP.is_equal)
            p3 = ps(tile("s3", h), 0, n)
            mms("s3" + x, [(p3, ap("ib"), c("tf", h, 3, 0, n)), (p3, ap("s3m"), c("sr", h))])
            tt("sv" + x, zq(h, 1), p3, s4, OP.is_equal)
        for h in range(H):
            x = ".%d" % h
            sv, es = zq(h, 1), c("es", h)
            pt = ps(tile("t", h), 0, n)
            mms("t" + x, [(pt, ap("tm"), sv)])
            lin("tr" + x, "S", c("tr", h), pt, 1.0, col(7), True)
            pk = ps(tile("k", h), 0, n)
            mms("k" + x, [(pk, ap("u4k"), sv), (pk, ap("ib"), es), (pk, ap("n4k"), c("tr", h))])
            pf = ps(tile("g", h), 0, n)
            if cfg["sort"][h] == "F":
                lin("ra" + x, "S", c("rr", h, 15, 0, n), pk, 1.0, col(21), True)
                lin("rb" + x, "S", c("rr", h, 15, n, 2 * n), pk, 1.0, col(22), True)
                lin("rc" + x, "S", c("rr", h, 15, 2 * n, 4 * n), c("rr", h, 15, 0, 2 * n), 1.0, -8192.0, True)
                lin("rd" + x, "S", c("rr", h, 15, 4 * n, 8 * n), c("rr", h, 15, 0, 4 * n), 1.0, -16384.0, True)
                lin("re" + x, "S", c("rr", h, 15, 8 * n, 12 * n), c("rr", h, 15, 0, 4 * n), 1.0, -32768.0, True)
                lin("rf" + x, "S", c("rr", h, 15, 12 * n, 15 * n), c("rr", h, 15, 0, 3 * n), 1.0, -49152.0, True)
                tl = tile("f", h)
                fm = [(ps(tl, 0, n), es, ap("o1", 15, 143))] + [(ap3(tl, slice(0, 8), slice(p - 1, p + 1)), c("rr", h, 15, n * p - n, n * p), ap("pm"))
                                                               for p in range(1, 16)]
                mms("fa" + x, fm[:5], True, False)
                mms("fb" + x, fm[5:9], False, False)
                mms("fc" + x, fm[9:13], False, False)
                mms("fd" + x, fm[13:], False, True)
                lin("ft" + x, "S", c("ft", h), ps(tl, 0, n))
                mms("fe" + x, [(pf, c("ft", h), ap("idf"))])
                lin("fv" + x, "S", c("fv", h), pf, 1.0, col(10))
            else:
                ts("ra" + x, c("ua", h, 2, 0, n), pk, col(23), 32768.0, OP.add, OP.min)
                lin("rb" + x, "V", c("ua", h, 2, n, 2 * n), pk, 1.0, col(14), True)
                for nm, src, dst, m, w in (("rc", "ua", "ub", 2, 16384.0), ("rd", "ub", "uc", 4, 8192.0)):
                    ts(nm + "0" + x, c(dst, h, 2 * m, 0, m * n), c(src, h, m), w, None, OP.min)
                    ts(nm + "1" + x, c(dst, h, 2 * m, m * n, 2 * m * n), c(src, h, m), -w, None, OP.add)
                ts("re0" + x, c("ud", h, 16, 0, 8 * n), c("uc", h, 8), 4096.0, -2048.0, OP.min, OP.add)
                ts("re1" + x, c("ud", h, 16, 8 * n, 16 * n), c("uc", h, 8), 4096.0, -6144.0, OP.max, OP.add)
                for j in range(2):
                    lst = []
                    for i in range(8 * j, 8 * j + 8):
                        p = int("{:04b}".format(i)[::-1], 2)
                        lst.append((pf, ap("o1", 15 - p, 143 - p), c("ud", h, 16, n * i, n * i + n)))
                    mms("f%s" % "ab"[j] + x, lst, j == 0, j == 1)
                lin("fv" + x, "S", c("fv", h), pf, 1.0, col(14))
            pq = ps(tile("q", h), 0, n)
            mms("q" + x, [(pq, ap("ib"), c("hf", h)), (pq, ap("qa"), sv)])
            ts("q1" + x, zq(h, 0), pq, -4096.0, -2048.0, OP.add, OP.max)
        pl = ps(tile("l", 0), 0, 48)
        mms("l", [(pl, ap("o1", 15 - b, 143 - b), ap("zq", 768 * t + b, 768 * t + 768, 16)) for b in range(16)])
        lin("ui", "V", ap("ui", 0, 48), pl)
        ts("uj", ap("ui", 32, 48), ap("ui", 32, 48), 15, None, OP.bitwise_and)
        ts("uk", ap("ui", 48, 64), ap("ui", 0, 16), 3840, None, OP.bitwise_and)
        tt("lc", ap("l2"), ap("ui"), ap("stat"), OP.add)
        if not last:
            op("ns", "S", ("act", ap("junk"), ap("ui", 16, 32), AF.Relu, 64.0, -32.0, ap("acol", 0, 1)))
            lin("av", "V", ap("av"), ap("ones", 0, n), ap("acol", 0, 1), -20352.0)
        for h in range(H):
            x = ".%d" % h
            sv, es = zq(h, 1), c("es", h)
            op("cs" + x, "V", ("copy", ind(c("cf", h, 16), ap("l2", 32 + 8 * h, 40 + 8 * h)), c("fv", h)))
            svb = sv[2][1].start
            zn = c("zo", h) if last else ap("zs", 256 * t + n * h, 256 * t + n * h + n)
            for j in range(4):
                jj = "%d%d" % (j // 2, j % 2)
                tl = tile("x" + jj, h)
                mms("x" + jj + x, [(ap3(tl, ALL, slice(0, 1)), ap("n256"), ap("twos"))] +
                    [(ap3(tl, ALL, slice(i, i + 1)), ap("rs", 128 * i - 128, 128 * i), ap("zq", svb + 32 * j, svb + 32 * j + 32))
                     for i in range(1, 16)])
                part = (h, 16, 512 * j, 512 * j + 512)
                d = ps(tl, 0, 512)
                if jj + x in cfg["via"]:
                    lin("xd" + jj + x, "S", c("xd", *part), d)
                    d = c("xd", *part)
                op("xs" + jj + x, "V", ("scan", c("xs", *part), d, c("xw", *part), 0.0, OP.add, OP.max))
            pz = ps(tile("zb", h), 0, n)
            mms("xb" + x, [(pz, ap("n256"), ap("ones", 0, n)), (pz, ap("rs", 128 * 15, 128 * 16), sv)])
            tt("zn" + x, zn, pz, c("xs", h, 16, 15, 2048, 16), OP.add)
            py = ps(tile("y", h), 0, n)
            sn = c("ysf", h) if last else ap("ss", 256 * t + n * h, 256 * t + n * h + n)
            mms("y" + x, [(py, ap("ib"), es), (py, ap("i4k"), sv)])
            lin("yl" + x, "S", c("yl", h), py, 1.0, -2040.0, True)
            gather("ya", h, "ya", ap("mt"), c("yl", h), 0, 4)
            for p in range(2):
                part = (h, 16, 1024 * p, 1024 * p + 1024)
                op("yn%d" % p + x, "V", ("scan", c("yn", *part), ap("rx"), c("ya", *part), -4096.0, OP.add, OP.max))
            lin("sn" + x, "V", sn, c("yn", h, 16, 15, 2048, 16), 1.0, 2047.0)
            if last:
                op("o.s" + x, "Y", ("dma", ap("ys", n * h, n * h + n), c("ysf", h)))
                op("o.z" + x, "Y", ("dma", ap("yz", n * h, n * h + n), zn))
            else:
                op("ms" + x, "G", ("send", ap("su", 256 * t + 256 + n * h, 256 * t + 256 + n * h + n), sn, 4 * t + 2 * h))
                op("mz" + x, "G", ("send", zq(h, 2, t + 1), zn, 4 * t + 2 * h + 1))
        if not last:
            tt("si", ap("si"), ind(ap("xt"), ap("l2", 0, 16)), ap("zs", 256 * t, 256 * t + 256), OP.add)
            lin("sj", "V", ap("sj"), ap("si"), 0.5, -0.25)
            op("xc", "V", ("copy", ind(ap("xt"), ap("l2", 48, 64)), ap("sj")))
        else:
            mms("yx", [(ps("P:yx", 0, 256), ap("mi", 128 * m, 128 * m + 128), ap("xt", 256 * m, 256 * m + 256)) for m in range(16)])
            lin("oyx", "S", ap("oyx"), ps("P:yx", 0, 256))
            for h in range(H):
                x = ".%d" % h
                tt("si" + x, c("si", h), ind(ap("xt"), ap("l2", 8 * h, 8 * h + 8)), c("zo", h), OP.add)
                lin("sj" + x, "V", c("sj", h), c("si", h), 0.5, -0.25)
                pw = ps(tile("w", h), 0, n)
                mms("wp" + x, [(pw, ap("ob"), zq(h, 0))])
                lin("wq" + x, "V", c("hh", h), pw, 1.0 / 256, 128.5 + 1.0 / 512)
                tt("dl" + x, c("p1", h), ind(ap("xt"), ap("l2", 48 + 8 * h, 56 + 8 * h)), c("sj", h), OP.subtract)
                tt("dm" + x, c("p1", h), c("p1", h), c("hh", h), OP.mult)
                tt("dn" + x, c("oyx", h), c("oyx", h), c("p1", h), OP.subtract)
                op("o.x" + x, "Y", ("dma", ap("yx", n * h, n * h + n), c("oyx", h)))
            for h in range(H):
                x = ".%d" % h
                for j in range(2):
                    name = "ch%d" % j + x
                    o, i = c("gw", h, 16, 1024 * j, 1024 * j + 1024), c("cf", h, 16, 1024 * j, 1024 * j + 1024)
                    if cfg["eng"].get(name, "G") == "G":
                        sel(name, o, i, [[0, 1024]], OP.is_ge, 0, 0)
                    else:
                        lin(name, "S", o, i)
                    mms("yc%d" % j + x, [(ps("P:yc", 0, 256), ap("mi", 128 * m, 128 * m + 128), ap("gw", 256 * m, 256 * m + 256))
                                         for m in range(8 * h + 4 * j, 8 * h + 4 * j + 4)], h + j == 0, h + j == 2)
            lin("oyc", "S", ap("oyc"), ps("P:yc", 0, 256), 1.0, 2048.0 * 136)
            op("o.c", "A", ("dma", ap("yc"), ap("oyc")))
    return ops


def touches(o):
    rd, wr = [], []

    def add(lst, a):
        cs = cols(a)
        lst.append((a[1], int(cs.min()), int(cs.max())))

    for cl in o["calls"]:
        outs = [1, 6] if cl[0] == "act" else [1]
        for i, a in enumerate(cl):
            if not isap(a):
                continue
            if a[0] == "ind":
                add(wr if i in outs else rd, a[1])
                add(rd, a[2])
            else:
                add(wr if i in outs else rd, a)
    return rd, wr


def edges(ops):
    seen = {}
    preds = []
    for i, o in enumerate(ops):
        rd, wr = touches(o)
        p = {}
        for lst, w in ((rd, False), (wr, True)):
            for (b, lo, hi) in lst:
                if b in DRAM:
                    continue
                psum = b.startswith("P:")
                for (j, lo2, hi2, w2) in seen.get(b, []):
                    if j == i:
                        continue
                    if psum:
                        p[j] = max(p.get(j, 0), 1 if (w2 and not w) else 0)
                    elif (w or w2) and lo <= hi2 and lo2 <= hi:
                        p[j] = 1
        for lst, w in ((rd, False), (wr, True)):
            for (b, lo, hi) in lst:
                seen.setdefault(b, []).append((i, lo, hi, w))
        preds.append(p)
        o["tiles"] = sorted(set(b for (b, _l, _h) in rd + wr if b.startswith("P:")))
    return preds


def queue_of(e):
    return "S" if e == "A" else e


def ranks(ops, names):
    pos = {}
    for i, nm in enumerate(names):
        key = nm.lstrip("+-")
        pos[key] = i + len(names) * (nm.count("+") - nm.count("-"))
    return [pos.get("%s@%d" % (o["key"], o["t"]), pos.get(o["key"], 0)) + len(names) * o["t"] for o in ops]


def arrange(ops, preds, rank):
    N = len(ops)
    succ = [[] for _ in range(N)]
    left = [len(p) for p in preds]
    for i in range(N):
        for j in preds[i]:
            succ[j].append(i)
    ready = [i for i in range(N) if left[i] == 0]
    order = []
    while ready:
        i = min(ready, key=lambda v: (rank[v], v))
        ready.remove(i)
        order.append(i)
        for s in succ[i]:
            left[s] -= 1
            if left[s] == 0:
                ready.append(s)
    return order


def pool(tile):
    return range(FLAT) if tile[2] == "x" else range(FLAT, 8) if tile[2] == "f" else range(8)


def banks(ops, order):
    lastuse = {}
    for p, i in enumerate(order):
        for b in ops[i]["tiles"]:
            lastuse[b] = p
    until, bank = [-1] * 8, {}
    for p, i in enumerate(order):
        for b in ops[i]["tiles"]:
            if b not in bank:
                k = min(pool(b), key=lambda v: until[v])
                assert until[k] < p
                bank[b] = k
                until[k] = lastuse[b]
    return bank


def with_banks(ops, preds, order, bank):
    full = [dict(p) for p in preds]
    users, lastt = {}, {}
    for i in range(len(ops)):
        for b in ops[i]["tiles"]:
            users.setdefault(b, []).append(i)
    for i in order:
        for b in ops[i]["tiles"]:
            if users[b][0] == i:
                if bank[b] in lastt:
                    for u in users[lastt[bank[b]]]:
                        full[i][u] = max(full[i].get(u, 0), 0)
                lastt[bank[b]] = b
    return full


def waits(ops, full, order):
    pos, cnt = {}, {}
    where = {i: p for p, i in enumerate(order)}
    for i in order:
        o = ops[i]
        own = o["eng"] in "YA" or o["calls"][0][0] == "send"
        key = ("own", i) if own else o["eng"]
        cnt[key] = cnt.get(key, 0) + 1
        pos[i] = (key, cnt[key])
    known = {}
    clock = {}
    need = {}
    for i in order:
        q = queue_of(ops[i]["eng"])
        kn = known.setdefault(q, {})
        want = {}
        for j, kind in full[i].items():
            key, p = pos[j]
            if key == ops[i]["eng"] and (kind == 0 or key == "P"):
                continue
            if kn.get(key, 0) < p and want.get(key, (0, 0))[0] < p:
                want[key] = (p, j)
        lst = []
        for key, (p, j) in sorted(want.items(), key=lambda kv: -where[kv[1][1]]):
            if kn.get(key, 0) >= p:
                continue
            lst.append(j)
            for k2, p2 in clock[j].items():
                if kn.get(k2, 0) < p2:
                    kn[k2] = p2
        need[i] = lst
        key, p = pos[i]
        if ops[i]["calls"][0][0] == "send":
            clock[i] = {key: p}
        else:
            clock[i] = dict(kn)
            clock[i][key] = p
    return need


PLAN = {}


def plan():
    if not PLAN:
        ops = build(CFG)
        preds = edges(ops)
        order = arrange(ops, preds, ranks(ops, ROUND.split()))
        bank = banks(ops, order)
        PLAN["p"] = (ops, order, bank, waits(ops, with_banks(ops, preds, order, bank), order))
    return PLAN["p"]


def lanes_engines(topo, src, dst):
    e = topo.engines(src, dst)
    return e[::max(1, len(e) // CFG["ne"])]


def rank_program(g, core, T, topo):
    rank = T.rank_of(core)
    if rank is None:
        return
    ops, order, bank, need = plan()
    nxt = T.cores[(rank + 1) % len(T.cores)]
    prv = T.cores[(rank - 1) % len(T.cores)]
    assert topo.may_write(core, nxt)
    out_eng = lanes_engines(topo, core, nxt)
    rid, pid = topo.addr(nxt)[0:2]
    Q = {"V": g.vector, "S": g.scalar, "P": g.tensor, "G": g, "Y": g.sync, "A": g.scalar}

    def R(a):
        if not isap(a):
            return a
        if a[0] == "ind":
            return R(a[1]).indirect(R(a[2]))
        if not a[1].startswith("P:"):
            return T[a[1]][a[2]]
        if bank[a[1]] >= FLAT:
            return T["ps%d" % bank[a[1]]][a[2]]
        cs = cols(a)
        step = int(cs[1] - cs[0])
        assert (np.diff(cs) == step).all()
        return T["ps%d" % bank[a[1]]][:, int(cs[0]):int(cs[-1]) + 1:step]

    waited = set(j for i in order for j in need[i])
    sig, cnt, nd, sent = {}, {}, [0], [0]
    for i in order:
        o = ops[i]
        q = Q[o["eng"]]
        for j in need[i]:
            q.wait_ge(T.sem[sig[j][0]], sig[j][1])
        ins = None
        for cl in o["calls"]:
            k, a = cl[0], [R(v) for v in cl[1:]]
            if k == "mm":
                ins = q.matmul(*a)
            elif k == "ts":
                ins = q.tensor_scalar(*a[:5]) if a[5] is None else q.tensor_scalar(*a)
            elif k == "tt":
                ins = q.tensor_tensor(*a)
            elif k == "copy":
                ins = q.tensor_copy(*a)
            elif k == "memset":
                ins = q.memset(*a)
            elif k == "scan":
                ins = q.tensor_tensor_scan(*a)
            elif k == "act":
                ins = q.activation(a[0], a[1], a[2], bias=a[3], scale=a[4], accum_out=a[5])
            elif k == "iota":
                if shape_of(cl[1][1])[1] == I32:
                    ins = q.iota(*a)
                else:
                    ins = q.iota(*a, allow_small_or_imprecise_dtypes=True)
            elif k == "sel":
                ins = q.affine_select(*a)
            elif k == "dma":
                ins = q.dma_start(a[0], a[1])
            elif k == "send":
                sem = "ar%d" % a[2]
                q.remote_dma(a[0], a[1], T.sem[sem], T.sem.left, pid, rid, sum(1 << e for e in out_eng))
                sig[i] = (sem, len(lanes_engines(topo, prv, core)))
                sent[0] += len(out_eng)
        if o["eng"] in "YA":
            sig[i] = ("d%d" % nd[0], 16)
            nd[0] += 1
            ins.then_inc(T.sem[sig[i][0]], 16)
        elif i in waited and i not in sig:
            cnt[o["eng"]] = cnt.get(o["eng"], 0) + 1
            sig[i] = (o["eng"], cnt[o["eng"]])
            ins.then_inc(T.sem[o["eng"]], 1)
    g.wait_ge(T.sem.left, sent[0])
    for i in order:
        if ops[i]["eng"] in "YA" and i not in waited:
            g.sync.wait_ge(T.sem[sig[i][0]], 16)
